import numpy as np, ml_dtypes
CORES = [35,38,43,46]
N = 4
BF = ml_dtypes.bfloat16
def gentries(a):
    return np.ascontiguousarray(a.reshape(8, 16, -1).transpose(0, 2, 1)).reshape(8, -1)
def gtable(e):
    e = np.asarray(e); return np.ascontiguousarray(e.reshape(8, -1, 16).transpose(0, 2, 1)).reshape(128, -1).astype(np.int32)
V, B, BITS, RO = 2048, 512, 12, 5
M = N * B
W = M + V - B
C = 2 ** BITS
def seen(q, p):
    bq = np.ascontiguousarray(q[..., :B].transpose(1, 2, 0, 3)).reshape(8, 16, M)
    bp = np.ascontiguousarray(p[..., :B].transpose(1, 0, 2)).reshape(8, M)
    gs, qps, qgs = [], [], []
    for a in range(N):
        wq = np.concatenate([bq, q[a, :, :, B:]], axis=2); wp = np.concatenate([bp, p[a, :, B:]], axis=1)
        g = np.take_along_axis(wp, p[a], 1)
        gs.append(g); qps.append(np.take_along_axis(wq, p[a][:, None, :], 2)); qgs.append(np.take_along_axis(wq, g[:, None, :], 2))
    return np.stack(gs), np.stack(qps), np.stack(qgs)
def dots(am, z):
    return np.matmul(am.transpose(0, 1, 3, 2), z)
def codes(am, t, z):
    return np.add.reduce(np.where(dots(am, z)[:, :, :BITS] > t[:, :, :BITS], 2 ** np.arange(BITS)[:, None], 0), axis=2)
def forest(rng):
    span = rng.choice(np.array([2, 16, B, M]), (8, 1)); i = np.arange(M)
    o = np.argsort(rng.random((8, M)), axis=1); back = np.minimum(i, (rng.random((8, M)) * span).astype(np.int64) + 1)
    pb = np.zeros((8, M), np.int64); np.put_along_axis(pb, o, np.take_along_axis(o, i - np.where(rng.random((8, M)) < 0.02, 0, back), 1), 1)
    h = V - B; i = np.arange(h); span = rng.choice(np.array([2, 16, B, h]), (N, 8, 1))
    o = np.argsort(rng.random((N, 8, h)), axis=2); back = np.minimum(i, (rng.random((N, 8, h)) * span).astype(np.int64) + 1)
    pi = np.zeros((N, 8, h), np.int64); np.put_along_axis(pi, o, np.take_along_axis(o, i - np.where(rng.random((N, 8, h)) < 0.02, 0, back), 2), 2)
    pi = np.where(rng.random((N, 8, h)) < 0.5, rng.integers(0, M, (N, 8, h)), M + pi)
    return np.concatenate([pb.reshape(8, N, B).transpose(1, 0, 2), pi], axis=2)
def parts(rng):
    amp = rng.choice(np.array([8, 24, 64]), (N, 8, 1, V))
    q = 64 + np.floor((2 * rng.random((N, 8, 16, V)) - 1) * amp).astype(np.int64); q = np.clip(q, 0, 127)
    am = rng.integers(-1, 2, (N, 8, 16, 16))
    t = 128 * np.add.reduce(am, axis=2)[..., None] + rng.integers(-30, 31, (N, 8, 16, 1))
    c = np.clip(rng.choice(np.array([0, 8, 24, 64, 111]), (N, 8, 1, C)) + rng.integers(0, 17, (N, 8, 16, C)), 0, 127)
    return q, forest(rng), am, t, c
def pack(q, p, am, t, c):
    big = np.zeros((N, 128, 128), np.float32)
    for h in range(8): big[:, 16 * h:16 * h + 16, 16 * h:16 * h + 16] = am[:, h]
    return {"q": np.ascontiguousarray(q).reshape(N, 128, V).astype(np.float32).astype(BF), "par": np.stack([gtable(a) for a in p]), "amat": big.astype(BF),
            "clr": np.ascontiguousarray(c).reshape(N, 128, C).astype(np.float32).astype(BF), "th": np.ascontiguousarray(t).reshape(N, 128, 1).astype(np.int32)}
def setup_inputs(rng):
    return pack(*parts(rng))
def setup_inputs_edge(rng):
    q, p, am, t, c = parts(rng); q = 64 + rng.integers(-6, 7, q.shape)
    g, qp, qg = seen(q, p); s = dots(am, q + qg); low = rng.integers(0, 2, (N, 8, 16, 1)); low[:, :, 0] = 0; low[:, :, 1] = 1
    t = np.take_along_axis(s, rng.integers(0, V, (N, 8, 16, 1)), 3) - low
    code = codes(am, t, q + qg); gap = np.abs(q - qg)
    for a in range(N):
        for h in range(8):
            w = np.full(C, -1); w[code[a, h]] = np.arange(V); k = np.nonzero(w >= 0)[0]; n = np.arange(len(k))
            e = gap[a, h][:, w[k]].copy(); x = np.argmax(e, axis=0)
            e[x, n] = e[x, n] - ((rng.random(len(k)) < 0.5) & (e[x, n] > 0)).astype(np.int64)
            c[a, h][:, k] = e
    return pack(q, p, am, t, c)
def setup_inputs_chain(rng):
    q, p, am, t, c = parts(rng); k = np.arange(B)
    for r in range(N):
        p[r, 0::2, :B] = (r + 1) % N * B + (k + (r == N - 1)) % B
        p[r, 1::2, :B] = (r - 1) * B + k if r else np.where(k > 0, (N - 1) * B + k - 1, 0)
        p[r, :, B:] = M + np.arange(V - B) - 1; p[r, :, B] = r * B + B - 1
    c[:, 0:2] = 127; c[:, 2:4] = 0
    return pack(q, p, am, t, c)
def setup_inputs_alike(rng):
    q, p, am, t, c = parts(rng)
    p[:, 0:2, :B] = rng.choice(np.array([0, B - 1, B, M - 1]), (N, 2, B)); p[:, 0:2, B:] = rng.choice(np.array([0, M - 1, M, W - 1]), (N, 2, V - B))
    for r in range(N):
        p[r, 2, :B] = r * B + np.arange(B); p[r, 2, B:] = M + np.arange(V - B)
    p[:, 3, B:] = rng.integers(M, W, (N, V - B)); p[:, 4, B:] = rng.integers(0, M, (N, V - B))
    t[:, 5] = -4096; c[:, 5, :, C - 1] = rng.integers(20, 60, (N, 16)); t[:, 6] = 4096; c[:, 6, :, 0] = rng.integers(20, 60, (N, 16))
    q[:, 7] = 127 * rng.integers(0, 2, (N, 16, V)); one = np.arange(16)[:, None] == rng.integers(0, 16, (N, 1, C))
    c[:, 7] = 127 - (one & (rng.random((N, 1, C)) < 0.7)).astype(np.int64)
    return pack(q, p, am, t, c)
def setup_inputs_spread(rng):
    q, p, am, t, c = parts(rng)
    q = np.clip(np.floor(np.exp2(7.5 * rng.random((N, 8, 1, V))) * rng.random((N, 8, 16, V))).astype(np.int64), 0, 127)
    am = am * (rng.random((N, 8, 16, 16)) < rng.choice(np.array([0.1, 0.4, 1.0]), (N, 8, 1, 16)))
    t = np.floor(np.exp2(12 * rng.random((N, 8, 16, 1)) ** 1.5)).astype(np.int64) * rng.choice(np.array([-1, 1]), (N, 8, 16, 1)); t = np.clip(t, -4096, 4096)
    c = np.clip(np.floor(np.exp2(8 * rng.random((N, 8, 1, C))) * (0.5 + rng.random((N, 8, 16, C)))).astype(np.int64), 0, 127)
    return pack(q, p, am, t, c)
def setup_inputs_large(rng):
    q, p, am, t, c = parts(rng)
    q[:, :5] = 127 - np.floor(rng.random((N, 5, 16, V)) * rng.choice(np.array([1, 4, 16, 40]), (N, 5, 1, V))).astype(np.int64)
    cut = rng.integers(0, 3, (N, 5, 1, 16)); cut[:, 4] = 4; less = -rng.integers(0, 2, (N, 5, 16, 16)); less[:, 4] = -1
    sign = rng.choice(np.array([-1, 1]), (N, 5, 1, 16)); sign[:, 0] = 1; sign[:, 1] = -1
    am[:, :5] = sign * np.where(np.argsort(rng.random((N, 5, 16, 16)), axis=2) < cut, less, 1)
    for h in range(5, 8):
        a = int(rng.integers(0, N)); b = (a + 1) % N; ka = int(rng.integers(0, B)); kb = int(rng.integers(0, B))
        p[:, h] = a * B + ka; p[a, h, ka] = b * B + kb; p[b, h, kb] = b * B + kb
        am[:, h] = np.eye(16, dtype=np.int64); mid = rng.integers(32, 96, (N, 16, 1))
        for r in range(N):
            w = rng.permutation(np.concatenate([np.arange(C), rng.integers(0, C, max(V - C, 0))]))[:V]
            bit = (w[None, :] >> np.arange(16)[:, None]) & 1; bit[BITS:] = rng.integers(0, 2, (16 - BITS, V)); u = rng.random((16, V))
            q[r, h] = np.where(bit == 1, mid[r] + 1 + np.floor(u * (127 - mid[r])).astype(np.int64), np.floor(u * (mid[r] + 1)).astype(np.int64))
        t[:, h] = mid + q[b, h, :, kb][None, :, None]
    g, qp, qg = seen(q, p); s = np.take_along_axis(dots(am, q + qg), rng.integers(0, V, (N, 8, 16, 1)), 3)
    low = np.where((s & 3) == 1, 1, np.where((s & 3) == 3, 0, rng.integers(0, 2, s.shape)))
    t[:, :5] = (s - low)[:, :5]
    c[:] = 127 * rng.integers(0, 2, (N, 8, 1, C))
    return pack(q, p, am, t, c)
def check_inputs(d):
    bad = []
    for k in ("q", "clr"):
        x = np.asarray(d[k]).astype(np.float32)
        if not np.all((x >= 0) & (x <= 127) & (x == np.floor(x))): bad.append("numbers of " + k)
    if np.min(d["th"]) < -4096 or np.max(d["th"]) > 4096: bad.append("range of th")
    x = np.asarray(d["amat"]).astype(np.float32); same = np.arange(128)[:, None] // 16 == np.arange(128)[None, :] // 16
    if not np.all((x == 0) | (same & ((x == 1) | (x == -1)))): bad.append("numbers of amat")
    if np.min(d["par"]) < 0 or np.max(d["par"]) > W - 1: bad.append("range of par")
    if np.max(np.stack([gentries(a) for a in d["par"]])[:, :, :B]) > M - 1: bad.append("parents of border columns")
    return bad
def reference(q, par, amat, clr, th):
    x = q.astype(np.float32).astype(np.int64).reshape(N, 8, 16, V); p = np.stack([gentries(a) for a in par]).astype(np.int64)
    big = amat.astype(np.float32).astype(np.int64); am = np.stack([big[:, 16 * h:16 * h + 16, 16 * h:16 * h + 16] for h in range(8)], axis=1)
    c = clr.astype(np.float32).astype(np.int64).reshape(N, 8, 16, C); t = th.astype(np.int64).reshape(N, 8, 16, 1)
    for rnd in range(RO):
        g, xp, xg = seen(x, p)
        code = codes(am, t, x + xg)
        room = np.take_along_axis(c, code[:, :, None, :], 3)
        ok = np.all(room >= np.abs(x - xg), axis=2)
        p = np.where(ok, g, p); x = np.where(ok[:, :, None, :], x, (x + xp) >> 1)
    return {"yq": x.reshape(N, 128, V).astype(np.float32).astype(BF), "yp": np.stack([gtable(a) for a in p]).astype(np.float32)}

@@ -1,0 +1,479 @@
+from concourse.bass import DstId, RemoteDMATransfer
+from concourse.mybir import AluOpType, ActivationFunctionType
+
+N, V, B, RO = 4, 2048, 512, 5
+M = N * B
+W = M + V - B
+
+CHUNKS = [
+    {"c": (0, 512), "hb": "a256 v256", "e": "v256 a256", "ah": "a512", "ok": "v512", "nw": "a256 v256", "up": "v512"},
+    {"c": (512, 1280), "hb": "a768", "e": "v768", "ah": "v768", "ok": "v768", "nw": "a768", "up": "v768"},
+    {"c": (1280, 2048), "hb": "a256 a256 v256", "e": "a384 v384", "ah": "v768", "ok": "v768", "nw": "a384 a384", "up": "v384 v384"},
+]
+EPS = ["ps0", "ps1", "ps2"]
+SUMS = ["ps3", "ps4", "ps5", "ps6", "ps7"]
+
+SCRATCH = {}
+_BF, _FH, _F32, _I32, _U16 = "bfloat16", "float16", "float32", "int32", "uint16"
+for _nm, _n, _d in (
+        [(x, 128, _I32) for x in ("parI", "hiI", "loI", "lw")] + [(x, 128, _BF) for x in ("hib", "lob", "am", "am2", "idp", "idn")]
+        + [(x, V, _BF) for x in ("qraw", "yout")] + [("clrs", 4096, _BF), ("ones", 16, _BF), ("yb", 16 + 2048, _BF)]
+        + [(x, 144, _BF) for x in ("z", "zn", "zc")] + [("zh", 144, _FH)] + [(x, 1, _I32) for x in ("thI", "pI", "pmI")]
+        + [(x, 1, _F32) for x in ("thf", "thr", "thd", "pm", "pd", "wn")] + [(x, 8, _F32) for x in ("bias", "biasd", "rowg")]
+        + [(x, 16, _F32) for x in ("row", "oh", "pw", "pwo")] + [(x, 128, _F32) for x in ("own0", "own", "rowp")]
+        + [("hbh", B, _FH), ("mask", B, _BF), ("lo16", 32, _U16), ("hi16", 32, _U16)]
+        + [("Q%d" % k, W, _BF) for k in range(RO + 1)] + [("nf%d" % k, 128, _F32) for k in range(RO + 1)]
+        + [("nw%d" % k, W, _BF) for k in range(RO)] + [("n16_%d" % k, 128, _U16) for k in range(RO)]
+        + [("%s%d" % (x, k), V, _BF) for k in range(2) for x in ("hb", "bits", "okb", "e", "ae")]
+        + [("ah%d" % k, V, _FH) for k in range(2)] + [("af%d" % k, V, _F32) for k in range(2)]
+        + [("%s%d" % (x, k), 128, _F32) for k in range(2) for x in ("dn", "dh")]
+        + [("%s%d" % (x, k), 128, _U16) for k in range(2) for x in ("h16_", "c16_")]
+        + [("l34_%d" % k, 256, _F32) for k in range(2)] + [("l16_%d" % k, 256, _U16) for k in range(2)]):
+    SCRATCH[_nm] = ("sbuf", [128, _n], _d)
+for _k in range(8):
+    SCRATCH["ps%d" % _k] = ("psum", [128, 512], "float32")
+SEMAPHORES = ["sv", "sa", "sp", "sg", "ls", "al"] + ["%s%d" % (x, k) for x in ("an", "aq") for k in range(RO)] \
+    + ["%s%d" % (x, k) for x in ("ld", "st") for k in range(12)]
+QSEM = {"v": "sv", "a": "sa", "p": "sp", "g": "sg"}
+
+FAC, GEL, PE, WAKE, SAME, ISSUE, FLIGHT, DMA = 1.15, 1.56, 0.5, 90.0, 30.0, 700.0, 3000.0, 2000.0
+LEAD = {"0 gat hb": -20249, "i ts Q": -9028, "k0 c0": -2637, "0 act yout": -2259, "k0 c2": -3217, "0 tt dh": 24050, "0 act ae": -1574,
+        "2 gat hb": 1436, "0 gtt Q": -2179, "2 tc n16_": -5807, "i ms pw": -18957, "i ts thr": -4266, "0 tc h16_": 2660,
+        "1 tt l34_": 8487, "1 ts ah": -17644, "1 tc l16_": 10989, "k4 c2": -7641, "1 gat hb": -7582, "2 gtt Q": -1943, "k4 c0": -1459}
+
+
+def cost(kind, q, c):
+    if kind == "d":
+        return DMA + c[0]
+    if kind == "s":
+        return ISSUE
+    if kind == "n":
+        return FLIGHT
+    return FAC * (PE * c[1] if q == "p" else c[0] + 0.83 * (c[1] + GEL * c[2]))
+
+
+def add(G, q, c, reads, writes, fn, kind="c", sem=None, val=0, deps=(), tag=""):
+    i = len(G["ops"])
+    edges = {d: True for d in deps}
+    for kindrw, regs in ((0, reads), (1, writes)):
+        for (nm, c0, c1) in regs:
+            psum = nm[:2] == "ps"
+            for (a0, a1, o, w) in G["hist"].setdefault(nm, []):
+                other = psum and G["ops"][o]["q"] != q
+                if not other and (a0 >= c1 or c0 >= a1):
+                    continue
+                if w and not kindrw:
+                    edges[o] = True
+                elif kindrw or other:
+                    edges.setdefault(o, False)
+    for kindrw, regs in ((0, reads), (1, writes)):
+        for (nm, c0, c1) in regs:
+            h = G["hist"][nm]
+            psum = nm[:2] == "ps"
+            if kindrw:
+                h[:] = [x for x in h if not ((psum and q == "p") or (x[0] >= c0 and x[1] <= c1 and (
+                    not psum or x[2] == i or G["ops"][x[2]]["q"] == q)))]
+            h.append((c0, c1, i, kindrw))
+    lead = LEAD.get("%s %s" % (G["c"], tag), 0.0) + LEAD.get("k%d c%s" % (G["k"], G["c"]), 0.0)
+    G["ops"].append({"q": q, "cost": cost(kind, q, c), "fn": fn, "kind": kind, "sem": sem, "val": val, "edges": edges, "lead": lead})
+    return i
+
+
+def schedule(ops):
+    n = len(ops)
+    succ = [[] for _ in range(n)]
+    for i, o in enumerate(ops):
+        for d in o["edges"]:
+            succ[d].append(i)
+    step = lambda a, b: WAKE if ops[a]["q"] != ops[b]["q"] else SAME
+    way = [0.0] * n
+    for i in range(n - 1, -1, -1):
+        way[i] = ops[i]["cost"] + max([way[s] + step(i, s) for s in succ[i]] or [0.0])
+    pri = [w + o["lead"] for w, o in zip(way, ops)]
+    left = [len(o["edges"]) for o in ops]
+    ready, free = {}, {}
+    rt, start = [0.0] * n, [0.0] * n
+    for i in range(n):
+        if left[i] == 0:
+            ready.setdefault(ops[i]["q"], []).append(i)
+    for _ in range(n):
+        best = None
+        for q in sorted(ready):
+            lst = ready[q]
+            if not lst:
+                continue
+            first = min(rt[i] for i in lst)
+            s = first if q == "n" else max(free.get(q, 0.0), first)
+            if best is None or s < best[0]:
+                best = (s, q, max((i for i in lst if rt[i] <= s + 1e-9), key=lambda i: pri[i]))
+        s, q, c = best
+        ready[q].remove(c)
+        start[c] = s
+        f = s + ops[c]["cost"]
+        free[q] = s + 60.0 if ops[c]["kind"] == "d" else f
+        for x in succ[c]:
+            rt[x] = max(rt[x], f + step(c, x))
+            left[x] -= 1
+            if left[x] == 0:
+                ready.setdefault(ops[x]["q"], []).append(x)
+    return sorted(range(n), key=lambda i: (start[i], i))
+
+
+def build(g, core, T, topo):
+    A, F = AluOpType, ActivationFunctionType
+    r = T.rank_of(core)
+    G = {"ops": [], "hist": {}, "c": "i", "k": -1}
+    X = lambda nm, a, b, s=1: T[nm][:, a:b] if s == 1 else T[nm][:, a:b:s]
+    Y = lambda s: X(*s) if isinstance(s, tuple) else s
+    bare = lambda nm: nm.rstrip("0123456789")
+
+    def ts(out, in0, s1, op0, s2=None, op1=None, fast=False):
+        def fn():
+            if op1 is None:
+                return g.vector.tensor_scalar(X(*out), X(*in0), Y(s1), None, op0)
+            return g.vector.tensor_scalar(X(*out), X(*in0), Y(s1), Y(s2), op0, op1)
+        rd = [in0] + [s for s in (s1, s2) if isinstance(s, tuple)]
+        cyc = max(64.0, (in0[2] - in0[1]) * (0.5 if fast else 1.0))
+        return add(G, "v", (0, cyc, 0), rd, [out[:3]], fn, tag="ts " + bare(out[0]))
+
+    def tt(out, in0, in1, op):
+        cyc = max(64.0, (in0[2] - in0[1]) * (1.0 if "ps" in (in0[0][:2], in1[0][:2]) else 2.0))
+        return add(G, "v", (0, cyc, 0), [in0, in1], [out],
+                   lambda: g.vector.tensor_tensor(X(*out), X(*in0), X(*in1), op), tag="tt " + bare(out[0]))
+
+    def tc(out, in0):
+        return add(G, "v", (0, max(64.0, in0[2] - in0[1]), 0), [in0], [out],
+                   lambda: g.vector.tensor_copy(X(*out), X(*in0)), tag="tc " + bare(out[0]))
+
+    def ms(out, val):
+        return add(G, "v", (0, 64, 0), [], [out], lambda: g.vector.memset(X(*out), val), tag="ms " + bare(out[0]))
+
+    def act(out, in0, func, **kw):
+        rd = [in0] + [v for v in kw.values() if isinstance(v, tuple)]
+        return add(G, "a", (40, max(64.0, in0[2] - in0[1]), 0), rd, [out],
+                   lambda: g.scalar.activation(X(*out), X(*in0), func, **{nm: Y(v) for nm, v in kw.items()}),
+                   tag="act " + bare(out[0]))
+
+    def gat(q, out, win, off):
+        def fn():
+            w = X(*win).indirect(X(*off))
+            return g.vector.tensor_copy(X(*out), w) if q == "v" else g.scalar.activation(X(*out), w, F.Copy)
+        return add(G, q, (50 if q == "v" else 65, 0, out[2] - out[1]), [win, off], [out], fn, tag="gat " + bare(out[0]))
+
+    def gtt(out, win, off, in1, op):
+        return add(G, "v", (50, 0, out[2] - out[1]), [win, off, in1], [out],
+                   lambda: g.vector.tensor_tensor(X(*out), X(*win).indirect(X(*off)), X(*in1), op), tag="gtt " + bare(out[0]))
+
+    def mm(outs, lhs, rhs, start, stop):
+        return add(G, "p", (0, max(64, rhs[2] - rhs[1]), 0), [lhs, rhs], [outs],
+                   lambda: g.tensor.matmul(X(*outs), X(*lhs), X(*rhs), start, stop), tag="mm")
+
+    def ext(ps, zname, src, v0, v1):
+        w = (v1 - v0) // 16
+
+        def fn():
+            for i in range(16):
+                ins = g.tensor.matmul(T[ps][:, 0:w], T[zname][:, 15 - i:143 - i], T[src][:, v0 + i:v1:16], i == 0, i == 15)
+            return ins
+        return add(G, "p", (0, 16 * max(64, w), 0), [(zname, 0, 144), (src, v0, v1)], [(ps, 0, w)], fn, tag="ext " + bare(src))
+
+    def spread(ps, c0):
+        def fn():
+            for i in range(16):
+                o = T[ps][:, i:512:16]
+                g.tensor.matmul(o, T["yb"][:, 16 + 128 * i:144 + 128 * i], T["hib"][:, c0:c0 + 32], True, False)
+                ins = g.tensor.matmul(o, T["yb"][:, 15 + 128 * i:143 + 128 * i], T["lob"][:, c0:c0 + 32], False, True)
+            return ins
+        return add(G, "p", (0, 32 * 64, 0), [("yb", 0, 2064), ("hib", c0, c0 + 32), ("lob", c0, c0 + 32)], [(ps, 0, 512)], fn,
+                   tag="spread")
+
+    nst = [0]
+
+    def load(q, k, out, src, more=0.0):
+        eng = g.sync if q == "s" else g.scalar
+        return add(G, q, (more,), [], [out], lambda: eng.dma_start(X(*out), src), "d", "ld%d" % k, 16, tag="load")
+
+    def store(dst, src):
+        k = nst[0]
+        nst[0] += 1
+        return add(G, "s", (0.0,), [src], [], lambda: g.sync.dma_start(dst, X(*src)), "d", "st%d" % k, 16, tag="store")
+
+    peers = [c for c in T.cores if c != core]
+    near = [c for c in peers if topo.chip(c) == topo.chip(core)]
+    far = [c for c in peers if topo.chip(c) != topo.chip(core)]
+    efar = [e for e in topo.engines(core, far[0]) if all(e in topo.engines(core, c) for c in far)]
+    enear = [e for e in topo.engines(core, near[0]) if e not in efar]
+    nloc = [0]
+
+    def share(buf, sem, cols, step):
+        c0, c1 = cols
+
+        def fn():
+            tr = []
+            for dsts, eng in ((far, efar), (near, enear)):
+                ids = []
+                for c in dsts:
+                    rid, pid, se = topo.addr(c)
+                    ids.append(DstId(rid=rid, pnc=pid))
+                tr.append(RemoteDMATransfer(dst_ids=ids, dma_engine_mask=sum(1 << e for e in eng), remote_sem=T.sem[sem],
+                                            srcs=[X(buf, c0, c1)], dsts=[X(buf, c0, c1)] * len(ids)))
+            return g.remote_dma_fused(tr, local_sem=T.sem.ls)
+        nloc[0] += len(efar) + len(enear)
+        i = add(G, "g", (0.0,), [(buf, c0, c1)], [], fn, "s", tag="share " + bare(buf))
+        tot = 0
+        for c in peers:
+            f2 = [x for x in T.cores if topo.chip(x) != topo.chip(c)]
+            e2 = topo.engines(c, f2[0])
+            tot += len(e2) if topo.chip(c) != topo.chip(core) else len([e for e in topo.engines(c, core) if e not in e2])
+        wr = [(buf, a, b) for (a, b) in ((0, c0), (c1, N * step)) if b > a]
+        add(G, "n", (0.0,), [], wr, None, "n", sem, tot, deps=[i], tag="arr " + bare(buf))
+
+    def own(v0, v1):
+        o = r * B if v1 <= B else M - B
+        return (v0 + o, v1 + o)
+
+    mine = ("lw", 32 * r, 32 * r + 32)
+    load("s", 0, mine, T.par[:, 0:32])
+    load("a", 1, ("qraw", 0, B), T.q[:, 0:B])
+    load("s", 2, ("parI", 32, 128), T.par[:, 32:128])
+    load("s", 3, ("am", 0, 128), T.amat[:, :])
+    load("s", 4, ("thI", 0, 1), T.th[:, :])
+    load("s", 5, ("qraw", B, V), T.q[:, B:V], 1000.0)
+    load("s", 6, ("clrs", 0, 4096), T.clr[:, :], 3000.0)
+
+    def io(out, pattern, base, cm, flag):
+        kw = {"allow_small_or_imprecise_dtypes": True} if flag else {}
+        return add(G, "g", (130, 2 * (out[2] - out[1]), 0), [], [out], lambda: g.iota(X(*out), pattern, base, cm, **kw), tag="iota")
+    io(("pI", 0, 1), [[0, 1]], 0, 1, False)
+    io(("rowg", 0, 8), [[16, 8]], 0, 0, True)
+    io(("row", 0, 16), [[1, 16]], 0, 0, True)
+    io(("own0", 0, 32), [[16, 32]], r * B, 0, True)
+    io(("own0", 32, 128), [[16, 96]], M, 0, True)
+    io(("rowp", 0, 128), [[1, 128]], 0, -1, True)
+    ts(("pmI", 0, 1), ("pI", 0, 1), 15, A.bitwise_and)
+    tc(("pm", 0, 1), ("pmI", 0, 1))
+    tt(("pd", 0, 1), ("pI", 0, 1), ("pm", 0, 1), A.subtract)
+    ts(("oh", 0, 16), ("row", 0, 16), ("pm", 0, 1), A.is_equal)
+    ms(("z", 0, 144), 0.0)
+    ts(("z", 15, 128, 16), ("rowg", 0, 8), ("pd", 0, 1), A.is_equal)
+    tc(("zh", 0, 144), ("z", 0, 144))
+    ms(("yb", 0, 16), 0.0)
+    for i in range(16):
+        ts(("yb", 16 + 128 * i, 144 + 128 * i), ("z", 15, 143), ("oh", i, i + 1), A.mult, fast=True)
+
+    def names0(c0, c1):
+        src = mine if c0 == 0 else ("parI", c0, c1)
+        ts(("hiI", c0, c1), src, 4, A.arith_shift_right)
+        ts(("loI", c0, c1), src, 15, A.bitwise_and)
+        tc(("hib", c0, c1), ("hiI", c0, c1))
+        tc(("lob", c0, c1), ("loI", c0, c1))
+        if c0 == 0:
+            tc(("lo16", 0, 32), ("loI", 0, 32))
+            tc(("hi16", 0, 32), ("hiI", 0, 32))
+            for x in (0, 256):
+                gat("a" if x else "v", ("mask", x, x + 256), ("oh", 0, 16), ("lo16", x // 16, x // 16 + 16))
+        for b in range(c0, c1, 32):
+            ps = "ps%d" % (3 + (b // 32))
+            spread(ps, b)
+            a0, a1 = own(16 * b, 16 * b + 512)
+            act(("nw0", a0, a0 + 256), (ps, 0, 256), F.Copy)
+            if b == 0:
+                tc(("nw0", a0 + 256, a1), (ps, 256, 512))
+            else:
+                act(("nw0", a0 + 256, a1), (ps, 256, 512), F.Copy)
+    share("lw", "al", mine[1:], 32)
+    a0, a1 = own(0, B)
+    ts(("Q0", a0, a1), ("qraw", 0, B), 128.0, A.add, fast=True)
+    share("Q0", "aq0", own(0, B), B)
+    names0(0, 32)
+    share("nw0", "an0", own(0, B), B)
+    ts(("wn", 0, 1), ("oh", 0, 1), 16.0, A.mult, ("oh", 1, 2), A.add)
+    ms(("pw", 12, 16), 0.0)
+    for i in range(12):
+        ms(("pw", i, i + 1), float(2 ** i))
+    tt(("pwo", 0, 16), ("pw", 0, 16), ("oh", 0, 16), A.mult)
+    for h in (8, 4, 2, 1):
+        tt(("pwo", 0, h), ("pwo", 0, h), ("pwo", h, 2 * h), A.add)
+    ts(("zn", 0, 144), ("z", 0, 144), ("wn", 0, 1), A.mult, fast=True)
+    ts(("zc", 0, 144), ("z", 0, 144), ("pwo", 0, 1), A.mult, fast=True)
+    ts(("own", 0, 128), ("own0", 0, 128), ("pm", 0, 1), A.add)
+    ts(("idp", 0, 128), ("rowp", 0, 128), 0.0, A.is_equal)
+    ts(("idn", 0, 128), ("idp", 0, 128), -1.0, A.mult, fast=True)
+    for (c0, c1) in ((0, 32), (32, 128)):
+        src = mine if c0 == 0 else ("parI", c0, c1)
+        tc(("nf0", c0, c1), src)
+        tc(("n16_0", c0, c1), src)
+        tt(("dn0", c0, c1), ("nf0", c0, c1), ("own", c0, c1), A.subtract)
+    ms(("ones", 0, 16), 1.0)
+    mm(("ps7", 0, 2), ("am", 0, 128), ("ones", 0, 2), True, True)
+    tc(("thf", 0, 1), ("thI", 0, 1))
+    ts(("thr", 0, 1), ("ps7", 0, 1), 256.5, A.mult, ("thf", 0, 1), A.add)
+    ts(("thd", 0, 1), ("ps7", 0, 1), 256.0, A.mult, ("thf", 0, 1), A.add)
+    for k in range(RO):
+        ts(("bias", k, k + 1), ("thr", 0, 1), 0.5, A.add, -float(2 ** k), A.mult)
+        ts(("biasd", k, k + 1), ("thd", 0, 1), 0.5, A.add, -float(2 ** k), A.mult)
+    ts(("am2", 0, 128), ("am", 0, 128), 2.0, A.mult, fast=True)
+    names0(32, 128)
+    a0, a1 = own(B, V)
+    ts(("Q0", a0, a1), ("qraw", B, V), 128.0, A.add, fast=True)
+
+    sb = [0]
+
+    def bank():
+        sb[0] += 1
+        return SUMS[(sb[0] - 1) % len(SUMS)]
+
+    def cut(text, x):
+        out = []
+        for t in text.split():
+            out.append((x, x + int(t[1:]), t[0]))
+            x = out[-1][1]
+        return out
+
+    def halves(x, y):
+        m = -(-(y - x) // 512)
+        return [(x + (y - x) * j // m, x + (y - x) * (j + 1) // m) for j in range(m)]
+
+    for k in range(RO):
+        P = k % 2
+        Qk, Qn, Nk, e = "Q%d" % k, "Q%d" % (k + 1), "nw%d" % k, "e%d" % P
+        for ci, ch in enumerate(CHUNKS):
+            G["c"], G["k"] = str(ci), k
+            v0, v1 = ch["c"]
+            w0, w1 = v0 // 16, v1 // 16
+            w = w1 - w0
+            we = M if ci == 0 else W
+            eps = EPS[ci]
+            L = lambda nm: ("%s%d" % (nm, P), w0, w1)
+            H = lambda j: (eps, 128 * j, 128 * j + w)
+            S = lambda st: cut(ch[st], v0)
+            nf = ("nf%d" % k, w0, w1)
+            ah = ("af%d" if ch["ah"][0] == "a" else "ah%d") % P
+            if ci == 0 and k == 0:
+                for x, y, q in S("hb"):
+                    gtt(("hbh", x, y), ("lw", 0, M // 16), ("hi16", x // 16, y // 16), ("mask", x, y), A.mult)
+                ext(eps, "zh", "hbh", v0, v1)
+            else:
+                for x, y, q in S("hb"):
+                    gat(q, ("hb%d" % P, x, y), (Nk, 0, we), ("n16_%d" % k, x // 16, y // 16))
+                ext(eps, "zn", "hb%d" % P, v0, v1)
+            tc(L("h16_"), H(0))
+            tt(L("dh"), H(0), nf, A.subtract)
+            for x, y, q in S("ah"):
+                if q == "v":
+                    ts((ah, x, y), (Qk,) + own(x, y), -0.5 * 2 ** k, A.add, fast=True)
+                else:
+                    act((ah, x, y), (Qk,) + own(x, y), F.Identity, bias=-0.5 * 2 ** k)
+            for x, y, q in S("e"):
+                h16 = ("h16_%d" % P, x // 16, y // 16)
+                parts = [(bank(), x2, y2) for x2, y2 in halves(x, y)]
+                for ps, x2, y2 in parts:
+                    mm((ps, 0, y2 - x2), ("am2" if q == "v" else "am", 0, 128), (Qk,) + own(x2, y2), True, False)
+                if q == "v":
+                    gtt((e, x, y), (Qk, 0, we), h16, (ah, x, y), A.subtract)
+                else:
+                    gat("a", (e, x, y), (Qk, 0, we), h16)
+                for ps, x2, y2 in parts:
+                    mm((ps, 0, y2 - x2), ("am", 0, 128), (e, x2, y2), False, True)
+                    act(("bits%d" % P, x2, y2), (ps, 0, y2 - x2), F.Sign, bias=("bias" if q == "v" else "biasd", k, k + 1))
+            ext(eps, "zc", "bits%d" % P, v0, v1)
+            ts(L("c16_"), H(0), 0.5, A.mult, 2047.5, A.add)
+            for x, y, q in S("e"):
+                if q == "v":
+                    act(("ae%d" % P, x, y), (e, x, y), F.Abs, scale=float(2.0 ** -k), bias=-0.5)
+                    continue
+                for x2, y2 in halves(x, y):
+                    ps = bank()
+                    mm((ps, 0, y2 - x2), ("idn", 0, 128), (Qk,) + own(x2, y2), True, False)
+                    mm((ps, 0, y2 - x2), ("idp", 0, 128), (e, x2, y2), False, True)
+                    act(("ae%d" % P, x2, y2), (ps, 0, y2 - x2), F.Abs, scale=float(2.0 ** -k))
+            for x, y, q in S("ok"):
+                gtt(("okb%d" % P, x, y), ("clrs", 0, 4096), ("c16_%d" % P, x // 16, y // 16), ("ae%d" % P, x, y), A.is_ge)
+            ext(eps, "z", "okb%d" % P, v0, v1)
+            ts(H(1), H(0), 15.5, A.is_ge)
+            tt(H(2), H(1), L("dn"), A.mult)
+            l3, l4, l16 = ("l34_%d" % P, 2 * w0, w0 + w1), ("l34_%d" % P, w0 + w1, 2 * w1), "l16_%d" % P
+            if k < RO - 1:
+                tt(l4, H(2), ("own", w0, w1), A.add)
+                tc((l16, w0 + w1, 2 * w1), l4)
+                for x, y, q in S("nw"):
+                    o = w0 + w1 + (x - v0) // 16
+                    gat(q, ("nw%d" % (k + 1),) + own(x, y), (Nk, 0, we), (l16, o, o + (y - x) // 16))
+                if ci == 0:
+                    share("nw%d" % (k + 1), "an%d" % (k + 1), own(0, B), B)
+            tt(l3, nf, H(2), A.subtract)
+            tc((l16, 2 * w0, w0 + w1), l3)
+            for x, y, q in S("up"):
+                a0, a1 = own(x, y)
+                o = 2 * w0 + (x - v0) // 16
+                gtt((Qn, a0, a1), (Qk, 0, we), (l16, o, o + (y - x) // 16), (ah, x, y), A.add)
+                if k == RO - 1:
+                    h = (x + y) // 2
+                    act(("yout", x, h), (Qn, a0, a0 + h - x), F.Identity, scale=float(2.0 ** -RO), bias=-128.0)
+                    ts(("yout", h, y), (Qn, a0 + h - x, a1), 2.0 ** -RO, A.mult, -128.0, A.add, fast=True)
+                    store(T.yq[:, x:y], ("yout", x, y))
+            if k < RO - 1 and ci == 0:
+                share(Qn, "aq%d" % (k + 1), own(0, B), B)
+            tt(H(3), H(1), L("dh"), A.mult)
+            tt(("nf%d" % (k + 1), w0, w1), H(3), nf, A.add)
+            if k < RO - 1:
+                tc(("n16_%d" % (k + 1), w0, w1), ("nf%d" % (k + 1), w0, w1))
+                tt(("dn%d" % (1 - P), w0, w1), H(3), L("dn"), A.add)
+            else:
+                store(T.yp[:, w0:w1], ("nf%d" % RO, w0, w1))
+    return G, nloc[0]
+
+
+def rank_program(g, core, T, topo):
+    if T.rank_of(core) is None:
+        return
+    G, nloc = build(g, core, T, topo)
+    ops = G["ops"]
+    order = schedule(ops)
+    pos = [0] * len(ops)
+    for j, i in enumerate(order):
+        pos[i] = j
+    eng = {"v": g.vector, "a": g.scalar, "p": g.tensor, "g": g, "s": g.sync}
+    cnt = {"v": 0, "a": 0, "p": 0, "g": 0}
+    known = {q: {} for q in eng}
+    tok, snap = {}, {}
+
+    def wait(q, d):
+        s, v = tok[d]
+        k = known[q]
+        if k.get(s, 0) >= v:
+            return
+        eng[q].wait_ge(T.sem[s], v)
+        for a, b in snap[d].items():
+            if k.get(a, 0) < b:
+                k[a] = b
+    for i in order:
+        o = ops[i]
+        q = o["q"]
+        if o["kind"] == "n":
+            tok[i] = (o["sem"], o["val"])
+            snap[i] = {o["sem"]: o["val"]}
+            continue
+        for d in sorted(o["edges"], key=lambda d: -pos[d]):
+            if q == "p" and ops[d]["q"] == "p" and not o["edges"][d]:
+                continue
+            if ops[d]["kind"] != "s":
+                wait(q, d)
+        ins = o["fn"]()
+        if o["kind"] == "c":
+            cnt[q] += 1
+            tok[i] = (QSEM[q], cnt[q])
+            ins.then_inc(T.sem[QSEM[q]], 1)
+        elif o["kind"] == "d":
+            tok[i] = (o["sem"], o["val"])
+            ins.then_inc(T.sem[o["sem"]], 16)
+        if o["kind"] != "s":
+            snap[i] = dict(known[q])
+            snap[i][tok[i][0]] = tok[i][1]
+    g.wait_ge(T.sem.ls, nloc)
+    for i in range(len(ops)):
+        if ops[i]["kind"] in ("d", "n"):
+            wait("s", i)
+    for q in cnt:
+        if known["s"].get(QSEM[q], 0) < cnt[q]:
+            g.sync.wait_ge(T.sem[QSEM[q]], cnt[q])

@@ -1,60 +1,73 @@
+import math
+
 from concourse.bass import DstId, RemoteDMATransfer
 from concourse.mybir import AluOpType, ActivationFunctionType
 
 N, V, B, RO = 4, 2048, 512, 5
 M = N * B
 W = M + V - B
+LW = W // 16
+MID = W // 2
+GRANT, VETO = 16384, 32768
 
 CHUNKS = [
-    {"c": (0, 512), "hb": "a256 v256", "e": "v256 a256", "ah": "a512", "ok": "v512", "nw": "a256 v256", "up": "v512"},
-    {"c": (512, 1280), "hb": "a768", "e": "v768", "ah": "v768", "ok": "v768", "nw": "a768", "up": "v768"},
-    {"c": (1280, 2048), "hb": "a256 a256 v256", "e": "a384 v384", "ah": "v768", "ok": "v768", "nw": "a384 a384", "up": "v384 v384"},
+    {'c': (0, 512), 'mk': 'a512', 'ok': 'v512', 'sg': 'a512', 'ab': 'a512', 'l3': True, 'hb0': 'v512', 'hb': 'a512', 'e': 'a512', 'up': 'v512', 'ah': 'v', 'hf': 'v', 'out': 'v', 'e0': 'v384 a128', 'ah0': 'a', 'up4': 'v448 a64'},
+    {'c': (512, 1408), 'mk': 'a896', 'ok': 'v896', 'sg': 'a896', 'ab': 'a896', 'l3': False, 'hb0': 'v896', 'hb': 'v320 a576', 'e': 'a512 v384', 'up': 'v640 a256', 'ah': 'v', 'hf': 'v', 'out': 'a', 'e0': 'a896', 'ah0': 'a', 'up4': 'v608 a288', 'up0': 'v608 a288', 'e4': 'v512 a384'},
+    {'c': (1408, 2048), 'mk': 'a640', 'ok': 'v640', 'sg': 'a640', 'ab': 'a640', 'l3': False, 'hb0': 'v640', 'hb': 'a640', 'e': 'v512 a128', 'up': 'v640', 'ah': 'v', 'hf': 'v', 'out': 'a', 'e0': 'a640', 'ah0': 'a', 'up0': 'v288 a352', 'up4': 'v448 a192', 'hb4': 'v320 a320'},
 ]
-EPS = ["ps0", "ps1", "ps2"]
-SUMS = ["ps3", "ps4", "ps5", "ps6", "ps7"]
+MASKED = [(0, 0), (0, 1), (0, 2)]
+FILL = {"NB": "g512 g512 g512 g512", "NI": "v512 v512 g512 g512 g512 g512 g512 g512"}
+EPS = ["ps0", "ps2", "ps6"]
+DIST = ["ps1", "ps4", "ps4"]
 
 SCRATCH = {}
 _BF, _FH, _F32, _I32, _U16 = "bfloat16", "float16", "float32", "int32", "uint16"
 for _nm, _n, _d in (
-        [(x, 128, _I32) for x in ("parI", "hiI", "loI", "lw")] + [(x, 128, _BF) for x in ("hib", "lob", "am", "am2", "idp", "idn")]
-        + [(x, V, _BF) for x in ("qraw", "yout")] + [("clrs", 4096, _BF), ("ones", 16, _BF), ("yb", 16 + 2048, _BF)]
-        + [(x, 144, _BF) for x in ("z", "zn", "zc")] + [("zh", 144, _FH)] + [(x, 1, _I32) for x in ("thI", "pI", "pmI")]
-        + [(x, 1, _F32) for x in ("thf", "thr", "thd", "pm", "pd", "wn")] + [(x, 8, _F32) for x in ("bias", "biasd", "rowg")]
-        + [(x, 16, _F32) for x in ("row", "oh", "pw", "pwo")] + [(x, 128, _F32) for x in ("own0", "own", "rowp")]
-        + [("hbh", B, _FH), ("mask", B, _BF), ("lo16", 32, _U16), ("hi16", 32, _U16)]
-        + [("Q%d" % k, W, _BF) for k in range(RO + 1)] + [("nf%d" % k, 128, _F32) for k in range(RO + 1)]
-        + [("nw%d" % k, W, _BF) for k in range(RO)] + [("n16_%d" % k, 128, _U16) for k in range(RO)]
-        + [("%s%d" % (x, k), V, _BF) for k in range(2) for x in ("hb", "bits", "okb", "e", "ae")]
-        + [("ah%d" % k, V, _FH) for k in range(2)] + [("af%d" % k, V, _F32) for k in range(2)]
-        + [("%s%d" % (x, k), 128, _F32) for k in range(2) for x in ("dn", "dh")]
+        [(x, 128, _BF) for x in ("am", "idp", "kc", "kd", "ones")] + [(x, 128, _FH) for x in ("amh", "am2", "idn")]
+        + [(x, V, _BF) for x in ("qraw", "yout", "mask", "ub")] + [("clrs", 4096, _BF), ("oh", 16, _BF)]
+        + [(x, 144, _BF) for x in ("zv", "zc")] + [(x, 144, _FH) for x in ("zh", "zn")] + [(x, 128, _FH) for x in ("idh", "hf0", "hf1")]
+        + [(x, 1, _I32) for x in ("thI", "pI", "pmI")] + [(x, 1, _F32) for x in ("thf", "thd", "pm", "pd")]
+        + [(x, 8, _F32) for x in ("bias", "rowg")] + [(x, 16, _F32) for x in ("row", "pw", "p2")]
+        + [(x, 128, _F32) for x in ("own0", "own", "rowp", "pout")]
+        + [("LL", LW * RO, _I32), ("NB", M, _I32), ("NI", 4096, _I32), ("L0", LW, _F32)]
+        + [("Q%d" % k, W, _BF) for k in range(RO + 1)]
+        + [("%s%d" % (x, k), V, _BF) for k in range(2) for x in ("bits", "veto", "e", "ae")]
+        + [("%s%d" % (x, k), V, _FH) for k in range(2) for x in ("hb", "ah")]
         + [("%s%d" % (x, k), 128, _U16) for k in range(2) for x in ("h16_", "c16_")]
-        + [("l34_%d" % k, 256, _F32) for k in range(2)] + [("l16_%d" % k, 256, _U16) for k in range(2)]):
+        + [("y%d" % k, 512, _I32) for k in range(2)] + [("l16_%d" % k, 512, _U16) for k in range(2)]):
     SCRATCH[_nm] = ("sbuf", [128, _n], _d)
-for _k in range(8):
-    SCRATCH["ps%d" % _k] = ("psum", [128, 512], "float32")
-SEMAPHORES = ["sv", "sa", "sp", "sg", "ls", "al"] + ["%s%d" % (x, k) for x in ("an", "aq") for k in range(RO)] \
-    + ["%s%d" % (x, k) for x in ("ld", "st") for k in range(12)]
+SCRATCH["ps"] = ("psum", [128, 4096], "float32")
+SEMAPHORES = ["sv", "sa", "sp", "sg", "ls"] + ["%s%d" % (x, k) for x in ("an", "aq") for k in range(RO)] \
+    + ["%s%d" % (x, k) for x in ("ld", "st") for k in range(16)]
 QSEM = {"v": "sv", "a": "sa", "p": "sp", "g": "sg"}
 
-FAC, GEL, PE, WAKE, SAME, ISSUE, FLIGHT, DMA = 1.15, 1.56, 0.5, 90.0, 30.0, 700.0, 3000.0, 2000.0
-LEAD = {"0 gat hb": -20249, "i ts Q": -9028, "k0 c0": -2637, "0 act yout": -2259, "k0 c2": -3217, "0 tt dh": 24050, "0 act ae": -1574,
-        "2 gat hb": 1436, "0 gtt Q": -2179, "2 tc n16_": -5807, "i ms pw": -18957, "i ts thr": -4266, "0 tc h16_": 2660,
-        "1 tt l34_": 8487, "1 ts ah": -17644, "1 tc l16_": 10989, "k4 c2": -7641, "1 gat hb": -7582, "2 gtt Q": -1943, "k4 c0": -1459}
+COST = {"fac": 1.25, "gel": 1.56, "pe": 0.45, "wake": 90.0, "same": 30.0, "issue": 700.0, "flight": 1800.0, "col": 2.0, "dma": 2000.0,
+        "act": 90.0, "vec": 5.0}
+LEAD = {}
+PERIOD, PHASE = 125, {}
+TRIES, WARM, SEED = 80000, 400.0, 4
+ORDER = []
 
 
-def cost(kind, q, c):
+def cost(o, C):
+    kind, c = o["kind"], o["c"]
     if kind == "d":
-        return DMA + c[0]
+        return C["dma"] + c[0]
     if kind == "s":
-        return ISSUE
+        return C["issue"]
     if kind == "n":
-        return FLIGHT
-    return FAC * (PE * c[1] if q == "p" else c[0] + 0.83 * (c[1] + GEL * c[2]))
+        return C["flight"] + C["col"] * c[0]
+    more = C["act"] if o["q"] == "a" and not c[2] else C["vec"] if o["q"] == "v" else 0.0
+    return more + C["fac"] * (C["pe"] * c[1] if o["q"] == "p" else c[0] + 0.83 * (c[1] + C["gel"] * c[2]))
 
 
-def add(G, q, c, reads, writes, fn, kind="c", sem=None, val=0, deps=(), tag=""):
+def add(G, q, c, reads, writes, fn, kind="c", sem=None, val=0, deps=()):
     i = len(G["ops"])
     edges = {d: True for d in deps}
+    banks = lambda regs: [y for nm, a, b in regs for y in (
+        [("ps%d" % (int(nm[2:]) + j), max(a - 512 * j, 0), min(b - 512 * j, 512)) for j in range(a // 512, -(-b // 512))]
+        if nm[:2] == "ps" else [(nm, a, b)])]
+    reads, writes = banks(reads), banks(writes)
     for kindrw, regs in ((0, reads), (1, writes)):
         for (nm, c0, c1) in regs:
             psum = nm[:2] == "ps"
@@ -74,58 +87,150 @@ def add(G, q, c, reads, writes, fn, kind="c", sem=None, val=0, deps=(), tag=""):
                 h[:] = [x for x in h if not ((psum and q == "p") or (x[0] >= c0 and x[1] <= c1 and (
                     not psum or x[2] == i or G["ops"][x[2]]["q"] == q)))]
             h.append((c0, c1, i, kindrw))
-    lead = LEAD.get("%s %s" % (G["c"], tag), 0.0) + LEAD.get("k%d c%s" % (G["k"], G["c"]), 0.0)
-    G["ops"].append({"q": q, "cost": cost(kind, q, c), "fn": fn, "kind": kind, "sem": sem, "val": val, "edges": edges, "lead": lead})
+    G["ops"].append({"q": q, "c": c, "fn": fn, "kind": kind, "sem": sem, "val": val, "edges": edges,
+                     "keys": ("%s %s" % (G["c"], G["s"]), "k%d %s" % (G["k"], G["c"]))})
     return i
 
 
-def schedule(ops):
+def schedule(ops, C=COST, lead=LEAD):
     n = len(ops)
     succ = [[] for _ in range(n)]
     for i, o in enumerate(ops):
         for d in o["edges"]:
             succ[d].append(i)
-    step = lambda a, b: WAKE if ops[a]["q"] != ops[b]["q"] else SAME
+    step = lambda a, b: C["wake"] if ops[a]["q"] != ops[b]["q"] else C["same"]
+    ns = [cost(o, C) for o in ops]
     way = [0.0] * n
     for i in range(n - 1, -1, -1):
-        way[i] = ops[i]["cost"] + max([way[s] + step(i, s) for s in succ[i]] or [0.0])
-    pri = [w + o["lead"] for w, o in zip(way, ops)]
+        way[i] = ns[i] + max([way[s] + step(i, s) for s in succ[i]] or [0.0])
+    pri = [w + sum(lead.get(x, 0.0) for x in o["keys"]) for w, o in zip(way, ops)]
+    if PHASE:
+        pri = [-PERIOD * int(o["keys"][1].split()[0][1:]) - PHASE.get(o["keys"][0], 0) for o in ops]
     left = [len(o["edges"]) for o in ops]
-    ready, free = {}, {}
-    rt, start = [0.0] * n, [0.0] * n
-    for i in range(n):
-        if left[i] == 0:
-            ready.setdefault(ops[i]["q"], []).append(i)
-    for _ in range(n):
-        best = None
-        for q in sorted(ready):
-            lst = ready[q]
-            if not lst:
-                continue
-            first = min(rt[i] for i in lst)
-            s = first if q == "n" else max(free.get(q, 0.0), first)
-            if best is None or s < best[0]:
-                best = (s, q, max((i for i in lst if rt[i] <= s + 1e-9), key=lambda i: pri[i]))
-        s, q, c = best
-        ready[q].remove(c)
-        start[c] = s
-        f = s + ops[c]["cost"]
-        free[q] = s + 60.0 if ops[c]["kind"] == "d" else f
-        for x in succ[c]:
-            rt[x] = max(rt[x], f + step(c, x))
+    ready = [i for i in range(n) if left[i] == 0]
+    busy, start = {}, [0.0] * n
+    while ready:
+        i = max(ready, key=lambda x: (pri[x], -x))
+        ready.remove(i)
+        t = max([start[d] + ns[d] + step(d, i) for d in ops[i]["edges"]] or [0.0])
+        if ops[i]["kind"] != "n":
+            hold = 60.0 if ops[i]["kind"] == "d" else ns[i]
+            spans = busy.setdefault(ops[i]["q"], [])
+            for a, b in spans:
+                if b > t:
+                    if t + hold <= a:
+                        break
+                    t = b
+            spans.append((t, t + hold))
+            spans.sort()
+        start[i] = t
+        for x in succ[i]:
             left[x] -= 1
             if left[x] == 0:
-                ready.setdefault(ops[x]["q"], []).append(x)
+                ready.append(x)
     return sorted(range(n), key=lambda i: (start[i], i))
+
+
+def improve(ops, order, tries=TRIES, warm=WARM, seed=1, costs=(COST,)):
+    n, names = len(ops), "vapgsn"
+    q = [names.index(o["q"]) for o in ops]
+    pred = [set(o["edges"]) for o in ops]
+    ends = set(range(n)) - set().union(*pred)
+    sets = []
+    for C in costs:
+        ns = [cost(o, C) for o in ops]
+        lag = lambda a, b: C["wake"] if q[a] != q[b] else C["same"] if q[b] != 2 or ops[b]["edges"][a] else 0.0
+        sets.append((ns, [60.0 if o["kind"] == "d" else x for o, x in zip(ops, ns)], [[(d, lag(d, i)) for d in pred[i]] for i in range(n)]))
+    state = [seed]
+
+    def rnd():
+        state[0] = (state[0] * 6364136223846793005 + 1442695040888963407) % 2 ** 64
+        return (state[0] >> 11) / 2.0 ** 53
+
+    def run(S, order, j, old):
+        ns, hold, before = S
+        free, last = [0.0] * 6, [-1] * 6
+        fin, why = old[2][:], old[3][:]
+        miss = 5
+        for i in reversed(order[:j]):
+            if q[i] < 5 and last[q[i]] < 0:
+                last[q[i]], free[q[i]] = i, fin[i] - ns[i] + hold[i]
+                miss -= 1
+                if not miss:
+                    break
+        for i in order[j:]:
+            k = q[i]
+            t, w = free[k], -2 - last[k]
+            for d, lag in before[i]:
+                if fin[d] + lag >= t:
+                    t, w = fin[d] + lag, d
+            fin[i], why[i] = t + ns[i], w
+            if k < 5:
+                free[k], last[k] = t + hold[i], i
+        i = max(ends, key=lambda x: (fin[x], x))
+        return fin[i], i, fin, why
+    now = [run(S, order, 0, (0, 0, [0.0] * n, [0] * n)) for S in sets]
+    total = lambda rs: sum(x[0] for x in rs) / len(rs)
+    best = (total(now), order)
+    for it in range(tries):
+        _, i, _, why = now[int(rnd() * len(now))]
+        held = []
+        while why[i] != -1:
+            if why[i] < -1:
+                held.append(i)
+            i = why[i] if why[i] >= 0 else -2 - why[i]
+        i = held[int(rnd() * len(held))]
+        steps = int(-math.log(1.0 - rnd()) / 0.6)
+        a = b = order.index(i)
+        if rnd() < 0.6:
+            steps += 1
+            while a > 0 and steps:
+                a -= 1
+                steps -= q[order[a]] == q[i]
+            seg, moved, need = order[a:b + 1], {i}, set(pred[i])
+            for x in reversed(seg[:-1]):
+                if x in need:
+                    moved.add(x)
+                    need |= pred[x]
+            if seg[0] in moved:
+                continue
+            seg = [x for x in seg if x in moved] + [x for x in seg if x not in moved]
+        else:
+            a = order.index(-2 - why[i])
+            while b < n - 1 and steps:
+                b += 1
+                steps -= q[order[b]] == q[i]
+            seg = order[a:b + 1]
+            moved = {seg[0]}
+            for x in seg[1:]:
+                if pred[x] & moved:
+                    moved.add(x)
+            if i in moved:
+                continue
+            seg = [x for x in seg if x not in moved] + [x for x in seg if x in moved]
+        new = order[:a] + seg + order[b + 1:]
+        then = [run(S, new, a, old) for S, old in zip(sets, now)]
+        d = total(then) - total(now)
+        if d <= 0 or rnd() < math.exp(-d / (warm * (1.0 - it / tries) + 2.0)):
+            order, now = new, then
+            if total(now) < best[0]:
+                best = (total(now), order)
+    return best[1]
 
 
 def build(g, core, T, topo):
     A, F = AluOpType, ActivationFunctionType
     r = T.rank_of(core)
-    G = {"ops": [], "hist": {}, "c": "i", "k": -1}
-    X = lambda nm, a, b, s=1: T[nm][:, a:b] if s == 1 else T[nm][:, a:b:s]
+    G = {"ops": [], "hist": {}, "c": "i", "k": -1, "s": ""}
+
+    def X(nm, a, b, s=1):
+        if nm[:2] == "ps":
+            return T.ps[:, 512 * int(nm[2:]) + a:512 * int(nm[2:]) + b]
+        return T[nm][:, a:b] if s == 1 else T[nm][:, a:b:s]
     Y = lambda s: X(*s) if isinstance(s, tuple) else s
-    bare = lambda nm: nm.rstrip("0123456789")
+
+    def at(stage):
+        G["s"] = stage
 
     def ts(out, in0, s1, op0, s2=None, op1=None, fast=False):
         def fn():
@@ -133,70 +238,66 @@ def build(g, core, T, topo):
                 return g.vector.tensor_scalar(X(*out), X(*in0), Y(s1), None, op0)
             return g.vector.tensor_scalar(X(*out), X(*in0), Y(s1), Y(s2), op0, op1)
         rd = [in0] + [s for s in (s1, s2) if isinstance(s, tuple)]
-        cyc = max(64.0, (in0[2] - in0[1]) * (0.5 if fast else 1.0))
-        return add(G, "v", (0, cyc, 0), rd, [out[:3]], fn, tag="ts " + bare(out[0]))
+        return add(G, "v", (0, max(64.0, (in0[2] - in0[1]) * (0.5 if fast else 1.0)), 0), rd, [out[:3]], fn)
 
     def tt(out, in0, in1, op):
         cyc = max(64.0, (in0[2] - in0[1]) * (1.0 if "ps" in (in0[0][:2], in1[0][:2]) else 2.0))
-        return add(G, "v", (0, cyc, 0), [in0, in1], [out],
-                   lambda: g.vector.tensor_tensor(X(*out), X(*in0), X(*in1), op), tag="tt " + bare(out[0]))
+        return add(G, "v", (0, cyc, 0), [in0, in1], [out], lambda: g.vector.tensor_tensor(X(*out), X(*in0), X(*in1), op))
 
     def tc(out, in0):
-        return add(G, "v", (0, max(64.0, in0[2] - in0[1]), 0), [in0], [out],
-                   lambda: g.vector.tensor_copy(X(*out), X(*in0)), tag="tc " + bare(out[0]))
+        return add(G, "v", (0, max(64.0, in0[2] - in0[1]), 0), [in0], [out], lambda: g.vector.tensor_copy(X(*out), X(*in0)))
 
     def ms(out, val):
-        return add(G, "v", (0, 64, 0), [], [out], lambda: g.vector.memset(X(*out), val), tag="ms " + bare(out[0]))
+        return add(G, "v", (0, max(64.0, out[2] - out[1]), 0), [], [out], lambda: g.vector.memset(X(*out), val))
 
     def act(out, in0, func, **kw):
         rd = [in0] + [v for v in kw.values() if isinstance(v, tuple)]
         return add(G, "a", (40, max(64.0, in0[2] - in0[1]), 0), rd, [out],
-                   lambda: g.scalar.activation(X(*out), X(*in0), func, **{nm: Y(v) for nm, v in kw.items()}),
-                   tag="act " + bare(out[0]))
+                   lambda: g.scalar.activation(X(*out), X(*in0), func, **{nm: Y(v) for nm, v in kw.items()}))
 
-    def gat(q, out, win, off):
+    def gat(q, out, win, off, plus=0.0):
         def fn():
             w = X(*win).indirect(X(*off))
-            return g.vector.tensor_copy(X(*out), w) if q == "v" else g.scalar.activation(X(*out), w, F.Copy)
-        return add(G, q, (50 if q == "v" else 65, 0, out[2] - out[1]), [win, off], [out], fn, tag="gat " + bare(out[0]))
+            if q == "v":
+                return g.vector.tensor_scalar(X(*out), w, plus, None, A.add)
+            return g.scalar.activation(X(*out), w, F.Identity, bias=plus)
+        return add(G, q, (50 if q == "v" else 65, 0, out[2] - out[1]), [win, off], [out], fn)
 
     def gtt(out, win, off, in1, op):
         return add(G, "v", (50, 0, out[2] - out[1]), [win, off, in1], [out],
-                   lambda: g.vector.tensor_tensor(X(*out), X(*win).indirect(X(*off)), X(*in1), op), tag="gtt " + bare(out[0]))
+                   lambda: g.vector.tensor_tensor(X(*out), X(*win).indirect(X(*off)), X(*in1), op))
 
     def mm(outs, lhs, rhs, start, stop):
         return add(G, "p", (0, max(64, rhs[2] - rhs[1]), 0), [lhs, rhs], [outs],
-                   lambda: g.tensor.matmul(X(*outs), X(*lhs), X(*rhs), start, stop), tag="mm")
+                   lambda: g.tensor.matmul(X(*outs), X(*lhs), X(*rhs), start, stop))
 
-    def ext(ps, zname, src, v0, v1):
+    def ext(ps, zname, src, v0, v1, start=True, stop=True):
         w = (v1 - v0) // 16
 
         def fn():
             for i in range(16):
-                ins = g.tensor.matmul(T[ps][:, 0:w], T[zname][:, 15 - i:143 - i], T[src][:, v0 + i:v1:16], i == 0, i == 15)
+                ins = g.tensor.matmul(X(ps, 0, w), T[zname][:, 15 - i:143 - i], T[src][:, v0 + i:v1:16], start and i == 0,
+                                      stop and i == 15)
             return ins
-        return add(G, "p", (0, 16 * max(64, w), 0), [(zname, 0, 144), (src, v0, v1)], [(ps, 0, w)], fn, tag="ext " + bare(src))
+        return add(G, "p", (0, 16 * max(64, w), 0), [(zname, 0, 144), (src, v0, v1)], [(ps, 0, w)], fn)
 
-    def spread(ps, c0):
-        def fn():
-            for i in range(16):
-                o = T[ps][:, i:512:16]
-                g.tensor.matmul(o, T["yb"][:, 16 + 128 * i:144 + 128 * i], T["hib"][:, c0:c0 + 32], True, False)
-                ins = g.tensor.matmul(o, T["yb"][:, 15 + 128 * i:143 + 128 * i], T["lob"][:, c0:c0 + 32], False, True)
-            return ins
-        return add(G, "p", (0, 32 * 64, 0), [("yb", 0, 2064), ("hib", c0, c0 + 32), ("lob", c0, c0 + 32)], [(ps, 0, 512)], fn,
-                   tag="spread")
+    def io(out, pattern, base, cm, flag=True):
+        kw = {"allow_small_or_imprecise_dtypes": True} if flag else {}
+        return add(G, "g", (130, 2 * (out[2] - out[1]), 0), [], [out], lambda: g.iota(X(*out), pattern, base, cm, **kw))
 
-    nst = [0]
+    nd = {"ld": 0, "st": 0}
 
-    def load(q, k, out, src, more=0.0):
+    def dma(q, sem, reads, writes, dst, src, more=0.0):
         eng = g.sync if q == "s" else g.scalar
-        return add(G, q, (more,), [], [out], lambda: eng.dma_start(X(*out), src), "d", "ld%d" % k, 16, tag="load")
+        nd[sem] += 1
+        return add(G, q, (more,), reads, writes, lambda: eng.dma_start(dst, src), "d", "%s%d" % (sem, nd[sem] - 1), 16)
 
-    def store(dst, src):
-        k = nst[0]
-        nst[0] += 1
-        return add(G, "s", (0.0,), [src], [], lambda: g.sync.dma_start(dst, X(*src)), "d", "st%d" % k, 16, tag="store")
+    load = lambda q, out, src, more=0.0: dma(q, "ld", [], [out], X(*out), src, more)
+    store = lambda dst, src: dma("s", "st", [src], [], dst, X(*src))
+
+    def lay(win, src):
+        n = 16 * (src[2] - src[1])
+        return dma("s", "ld", [src], [(win, 0, n)], T[win][0:128:16, 0:n], X(*src))
 
     peers = [c for c in T.cores if c != core]
     near = [c for c in peers if topo.chip(c) == topo.chip(core)]
@@ -205,8 +306,8 @@ def build(g, core, T, topo):
     enear = [e for e in topo.engines(core, near[0]) if e not in efar]
     nloc = [0]
 
-    def share(buf, sem, cols, step):
-        c0, c1 = cols
+    def share(buf, sem, base, step, size):
+        c0, c1 = base + r * step, base + (r + 1) * step
 
         def fn():
             tr = []
@@ -219,109 +320,22 @@ def build(g, core, T, topo):
                                             srcs=[X(buf, c0, c1)], dsts=[X(buf, c0, c1)] * len(ids)))
             return g.remote_dma_fused(tr, local_sem=T.sem.ls)
         nloc[0] += len(efar) + len(enear)
-        i = add(G, "g", (0.0,), [(buf, c0, c1)], [], fn, "s", tag="share " + bare(buf))
+        i = add(G, "g", (0.0,), [(buf, c0, c1)], [], fn, "s")
         tot = 0
         for c in peers:
             f2 = [x for x in T.cores if topo.chip(x) != topo.chip(c)]
             e2 = topo.engines(c, f2[0])
             tot += len(e2) if topo.chip(c) != topo.chip(core) else len([e for e in topo.engines(c, core) if e not in e2])
-        wr = [(buf, a, b) for (a, b) in ((0, c0), (c1, N * step)) if b > a]
-        add(G, "n", (0.0,), [], wr, None, "n", sem, tot, deps=[i], tag="arr " + bare(buf))
+        wr = [(buf, a, b) for (a, b) in ((base, c0), (c1, base + N * step)) if b > a]
+        add(G, "n", (step * size // 2,), [], wr, None, "n", sem, tot, deps=[i])
 
     def own(v0, v1):
         o = r * B if v1 <= B else M - B
         return (v0 + o, v1 + o)
 
-    mine = ("lw", 32 * r, 32 * r + 32)
-    load("s", 0, mine, T.par[:, 0:32])
-    load("a", 1, ("qraw", 0, B), T.q[:, 0:B])
-    load("s", 2, ("parI", 32, 128), T.par[:, 32:128])
-    load("s", 3, ("am", 0, 128), T.amat[:, :])
-    load("s", 4, ("thI", 0, 1), T.th[:, :])
-    load("s", 5, ("qraw", B, V), T.q[:, B:V], 1000.0)
-    load("s", 6, ("clrs", 0, 4096), T.clr[:, :], 3000.0)
-
-    def io(out, pattern, base, cm, flag):
-        kw = {"allow_small_or_imprecise_dtypes": True} if flag else {}
-        return add(G, "g", (130, 2 * (out[2] - out[1]), 0), [], [out], lambda: g.iota(X(*out), pattern, base, cm, **kw), tag="iota")
-    io(("pI", 0, 1), [[0, 1]], 0, 1, False)
-    io(("rowg", 0, 8), [[16, 8]], 0, 0, True)
-    io(("row", 0, 16), [[1, 16]], 0, 0, True)
-    io(("own0", 0, 32), [[16, 32]], r * B, 0, True)
-    io(("own0", 32, 128), [[16, 96]], M, 0, True)
-    io(("rowp", 0, 128), [[1, 128]], 0, -1, True)
-    ts(("pmI", 0, 1), ("pI", 0, 1), 15, A.bitwise_and)
-    tc(("pm", 0, 1), ("pmI", 0, 1))
-    tt(("pd", 0, 1), ("pI", 0, 1), ("pm", 0, 1), A.subtract)
-    ts(("oh", 0, 16), ("row", 0, 16), ("pm", 0, 1), A.is_equal)
-    ms(("z", 0, 144), 0.0)
-    ts(("z", 15, 128, 16), ("rowg", 0, 8), ("pd", 0, 1), A.is_equal)
-    tc(("zh", 0, 144), ("z", 0, 144))
-    ms(("yb", 0, 16), 0.0)
-    for i in range(16):
-        ts(("yb", 16 + 128 * i, 144 + 128 * i), ("z", 15, 143), ("oh", i, i + 1), A.mult, fast=True)
-
-    def names0(c0, c1):
-        src = mine if c0 == 0 else ("parI", c0, c1)
-        ts(("hiI", c0, c1), src, 4, A.arith_shift_right)
-        ts(("loI", c0, c1), src, 15, A.bitwise_and)
-        tc(("hib", c0, c1), ("hiI", c0, c1))
-        tc(("lob", c0, c1), ("loI", c0, c1))
-        if c0 == 0:
-            tc(("lo16", 0, 32), ("loI", 0, 32))
-            tc(("hi16", 0, 32), ("hiI", 0, 32))
-            for x in (0, 256):
-                gat("a" if x else "v", ("mask", x, x + 256), ("oh", 0, 16), ("lo16", x // 16, x // 16 + 16))
-        for b in range(c0, c1, 32):
-            ps = "ps%d" % (3 + (b // 32))
-            spread(ps, b)
-            a0, a1 = own(16 * b, 16 * b + 512)
-            act(("nw0", a0, a0 + 256), (ps, 0, 256), F.Copy)
-            if b == 0:
-                tc(("nw0", a0 + 256, a1), (ps, 256, 512))
-            else:
-                act(("nw0", a0 + 256, a1), (ps, 256, 512), F.Copy)
-    share("lw", "al", mine[1:], 32)
-    a0, a1 = own(0, B)
-    ts(("Q0", a0, a1), ("qraw", 0, B), 128.0, A.add, fast=True)
-    share("Q0", "aq0", own(0, B), B)
-    names0(0, 32)
-    share("nw0", "an0", own(0, B), B)
-    ts(("wn", 0, 1), ("oh", 0, 1), 16.0, A.mult, ("oh", 1, 2), A.add)
-    ms(("pw", 12, 16), 0.0)
-    for i in range(12):
-        ms(("pw", i, i + 1), float(2 ** i))
-    tt(("pwo", 0, 16), ("pw", 0, 16), ("oh", 0, 16), A.mult)
-    for h in (8, 4, 2, 1):
-        tt(("pwo", 0, h), ("pwo", 0, h), ("pwo", h, 2 * h), A.add)
-    ts(("zn", 0, 144), ("z", 0, 144), ("wn", 0, 1), A.mult, fast=True)
-    ts(("zc", 0, 144), ("z", 0, 144), ("pwo", 0, 1), A.mult, fast=True)
-    ts(("own", 0, 128), ("own0", 0, 128), ("pm", 0, 1), A.add)
-    ts(("idp", 0, 128), ("rowp", 0, 128), 0.0, A.is_equal)
-    ts(("idn", 0, 128), ("idp", 0, 128), -1.0, A.mult, fast=True)
-    for (c0, c1) in ((0, 32), (32, 128)):
-        src = mine if c0 == 0 else ("parI", c0, c1)
-        tc(("nf0", c0, c1), src)
-        tc(("n16_0", c0, c1), src)
-        tt(("dn0", c0, c1), ("nf0", c0, c1), ("own", c0, c1), A.subtract)
-    ms(("ones", 0, 16), 1.0)
-    mm(("ps7", 0, 2), ("am", 0, 128), ("ones", 0, 2), True, True)
-    tc(("thf", 0, 1), ("thI", 0, 1))
-    ts(("thr", 0, 1), ("ps7", 0, 1), 256.5, A.mult, ("thf", 0, 1), A.add)
-    ts(("thd", 0, 1), ("ps7", 0, 1), 256.0, A.mult, ("thf", 0, 1), A.add)
-    for k in range(RO):
-        ts(("bias", k, k + 1), ("thr", 0, 1), 0.5, A.add, -float(2 ** k), A.mult)
-        ts(("biasd", k, k + 1), ("thd", 0, 1), 0.5, A.add, -float(2 ** k), A.mult)
-    ts(("am2", 0, 128), ("am", 0, 128), 2.0, A.mult, fast=True)
-    names0(32, 128)
-    a0, a1 = own(B, V)
-    ts(("Q0", a0, a1), ("qraw", B, V), 128.0, A.add, fast=True)
-
-    sb = [0]
-
-    def bank():
-        sb[0] += 1
-        return SUMS[(sb[0] - 1) % len(SUMS)]
+    def names(k, w0, w1):
+        a, b = own(16 * w0, 16 * w1)
+        return ("LL", LW * k + a // 16, LW * k + b // 16)
 
     def cut(text, x):
         out = []
@@ -331,96 +345,243 @@ def build(g, core, T, topo):
         return out
 
     def halves(x, y):
-        m = -(-(y - x) // 512)
-        return [(x + (y - x) * j // m, x + (y - x) * (j + 1) // m) for j in range(m)]
+        return [(a, min(a + 512, y)) for a in range(x, y, 512)]
+
+    def places(k, ci, first):
+        w0, w1 = [x // 16 for x in CHUNKS[ci]["c"]]
+        w, par = w1 - w0, names(k, w0, w1)
+        slot = lambda nm, j, n=1: ("%s%d" % (nm, (k + 1) % 2), 4 * w0 + j * w, 4 * w0 + (j + n) * w)
+        if (k, ci) in MASKED:
+            ts(slot("y", 2), par, 4, A.arith_shift_right)
+            ts(slot("y", 3), par, 15, A.bitwise_and)
+            tc(slot("l16_", 2, 2), slot("y", 2, 2))
+            for x, y, q in cut(CHUNKS[ci]["mk"], 16 * w0):
+                o = slot("l16_", 3)
+                gat(q, ("mask", x, y), ("oh", 0, 16), (o[0], o[1] + x // 16 - w0, o[1] + y // 16 - w0))
+            return
+        if ci == 0:
+            ts(slot("y", 2), par, 128.0625, A.mult, -15.0 / 32, A.add)
+        else:
+            ts(slot("y", 2), par, 256.0625, A.mult, (32 if k else 0) - 15.0 / 32 - 112 * 4096, A.add)
+        ts(slot("y", first, 3 - first), slot("y", first, 3 - first), M - 1 if ci == 0 else 4095, A.bitwise_and)
+        tc(slot("l16_", first, 3 - first), slot("y", first, 3 - first))
+
+    at("load")
+    load("s", names(0, 0, 32), T.par[:, 0:32])
+    load("a", ("qraw", 0, B), T.q[:, 0:B])
+    load("s", names(0, 32, 128), T.par[:, 32:128])
+    load("s", ("am", 0, 128), T.amat[:, :])
+    load("s", ("thI", 0, 1), T.th[:, :])
+    load("s", ("qraw", B, V), T.q[:, B:V], 1000.0)
+    load("s", ("clrs", 0, 4096), T.clr[:, :], 3000.0)
+    at("const")
+    io(("pI", 0, 1), [[0, 1]], 0, 1, False)
+    io(("rowg", 0, 8), [[16, 8]], 0, 0)
+    io(("row", 0, 16), [[1, 16]], 0, 0)
+    io(("own0", 0, 32), [[16, 32]], 4096 + r * B, 0)
+    io(("own0", 32, 128), [[16, 96]], 4096 + M, 0)
+    io(("rowp", 0, 128), [[1, 128]], 0, -1)
+    ts(("pmI", 0, 1), ("pI", 0, 1), 15, A.bitwise_and)
+    tc(("pm", 0, 1), ("pmI", 0, 1))
+    tt(("pd", 0, 1), ("pI", 0, 1), ("pm", 0, 1), A.subtract)
+    ts(("oh", 0, 16), ("row", 0, 16), ("pm", 0, 1), A.is_equal)
+    ms(("zv", 0, 144), 0.0)
+    ts(("zv", 15, 128, 16), ("rowg", 0, 8), ("pd", 0, 1), A.is_equal, -float(VETO), A.mult)
+    ts(("zh", 0, 144), ("zv", 0, 144), -1.0 / VETO, A.mult, fast=True)
+    ts(("zn", 0, 144), ("zh", 0, 144), ("oh", 0, 1), A.mult, fast=True) if False else None
+    ts(("thd", 0, 1), ("pm", 0, 1), 0.0, A.is_equal)
+    ts(("zn", 0, 144), ("zh", 0, 144), ("thd", 0, 1), A.mult, fast=True)
+    at("send")
+    share("LL", "an0", 0, 32, 4)
+    a0, a1 = own(0, B)
+    at("sendq")
+    ts(("Q0", a0, a1), ("qraw", 0, B), 128.0, A.add, fast=True)
+    share("Q0", "aq0", 0, B, 2)
+    at("lists")
+    for ci, ch in enumerate(CHUNKS):
+        places(0, ci, 2)
+    if (0, 1) in MASKED:
+        at("l0")
+        ts(("L0", 0, LW), ("LL", 0, LW), -float(MID), A.add)
+    at("const2")
+    ms(("p2", 0, 1), 1.0)
+    for h in (1, 2, 4, 8):
+        ts(("p2", h, min(2 * h, 12)), ("p2", 0, min(h, 12 - h)), float(2 ** h), A.mult)
+    ms(("p2", 12, 16), 0.0)
+    tt(("pw", 0, 16), ("p2", 0, 16), ("oh", 0, 16), A.mult)
+    for h in (8, 4, 2, 1):
+        tt(("pw", 0, h), ("pw", 0, h), ("pw", h, 2 * h), A.add)
+    ts(("zc", 0, 144), ("zh", 0, 144), ("pw", 0, 1), A.mult, fast=True)
+    ts(("own", 0, 128), ("own0", 0, 128), ("pm", 0, 1), A.add)
+    ts(("idp", 0, 128), ("rowp", 0, 128), 0.0, A.is_equal)
+    ts(("idn", 0, 128), ("rowp", 0, 128), 0.0, A.is_equal, -1.0, A.mult)
+    ts(("idh", 0, 128), ("rowp", 0, 128), 0.0, A.is_equal)
+    ms(("kc", 0, 128), (GRANT + MID) / 128.0)
+    ms(("kd", 0, 128), GRANT / 128.0)
+    ms(("ones", 0, 128), 1.0)
+    mm(("ps7", 0, 2), ("am", 0, 128), ("ones", 0, 2), True, True)
+    tc(("thf", 0, 1), ("thI", 0, 1))
+    ts(("thd", 0, 1), ("ps7", 0, 1), 255.5, A.mult, ("thf", 0, 1), A.add)
+    ts(("thd", 0, 1), ("thd", 0, 1), 0.5, A.add, -1.0, A.mult)
+    ts(("bias", 0, 8), ("p2", 0, 8), ("thd", 0, 1), A.mult)
+    ts(("amh", 0, 128), ("am", 0, 128), 1.0, A.mult, fast=True)
+    ts(("am2", 0, 128), ("am", 0, 128), 2.0, A.mult, fast=True)
+    a0, a1 = own(B, V)
+    at("q0")
+    ts(("Q0", a0, a1), ("qraw", B, V), 128.0, A.add, fast=True)
+    for win in sorted(FILL):
+        for x, y, q in cut(FILL[win], 0):
+            at("fill" + q)
+            if q == "v":
+                ms((win, x, y), 0.0)
+            else:
+                io((win, x, y), [[0, y - x]], 0, 0, False)
+
+    def decide(k, ci):
+        ch, P, last = CHUNKS[ci], k % 2, k == RO - 1
+        G["c"], G["k"] = str(ci), k
+        Qk, e = "Q%d" % k, "e%d" % P
+        v0, v1 = ch["c"]
+        w0, w1 = v0 // 16, v1 // 16
+        w = w1 - w0
+        we = M if ci == 0 else W
+        eps = EPS[ci]
+        L = lambda nm: ("%s%d" % (nm, P), w0, w1)
+        S = lambda st: cut(ch.get(st + str(k), ch[st]), v0)
+        slot = lambda nm, j, n=1, p=P: ("%s%d" % (nm, p), 4 * w0 + j * w, 4 * w0 + (j + n) * w)
+        par, ah = names(k, w0, w1), "ah%d" % P
+        whole = (k, ci) in MASKED and ci == 0
+        at("lay")
+        if (k, ci) not in MASKED and (ci < 2 or (k, 1) in MASKED):
+            if ci == 0:
+                lay("NB", ("LL", LW * k, LW * k + M // 16))
+            else:
+                lay("NI", ("LL", LW * (k + 1) - 256, LW * (k + 1)) if k else ("LL", 0, 256))
+        for x, y, q in S("hb"):
+            at("hb" + q)
+            o = slot("l16_", 2, 1, 1 - P)
+            o = (o[0], o[1] + x // 16 - w0, o[1] + y // 16 - w0)
+            if (k, ci) in MASKED:
+                gtt(("hb%d" % P, x, y), ("LL", LW * k, LW * k + M // 16) if whole else ("L0", 0, LW), o, ("mask", x, y), A.mult)
+            else:
+                gat(q, ("hb%d" % P, x, y), ("NB", 0, M) if ci == 0 else ("NI", 0, 4096), o, -float(MID))
+        at("xh")
+        ext(eps, "zh" if (k, ci) in MASKED else "zn", "hb%d" % P, v0, v1)
+        ts(L("h16_"), (eps, 0, w), 0.0 if whole else float(MID), A.add)
+        at("hf")
+        if ch["hf"] == "v":
+            tc(L("hf"), (eps, 0, w))
+        elif ch["hf"] == "a":
+            act(L("hf"), (eps, 0, w), F.Copy)
+        at("ah")
+        if ch.get("ah%d" % k, ch["ah"]) == "v":
+            ts((ah, v0, v1), (Qk,) + own(v0, v1), -0.5 * 2 ** k, A.add, fast=True)
+        else:
+            act((ah, v0, v1), (Qk,) + own(v0, v1), F.Identity, bias=-0.5 * 2 ** k)
+        got = lambda x, y, q: [(max(x, a), min(y, b)) for a, b, c in S("e") if c == q and max(x, a) < min(y, b)]
+        at("pre")
+        for x, y in halves(v0, v1):
+            mm((eps, x - v0, y - v0), ("amh" if got(x, y, "a") else "am2", 0, 128), (ah, x, y), True, False)
+            for a, b in got(x, y, "v") if got(x, y, "a") else []:
+                mm((eps, a - v0, b - v0), ("amh", 0, 128), (ah, a, b), False, False)
+        for x, y, q in S("e"):
+            h16 = ("h16_%d" % P, x // 16, y // 16)
+            at("e" + q)
+            if q == "v":
+                gtt((e, x, y), (Qk, 0, we), h16, (ah, x, y), A.subtract)
+            else:
+                gat("a", (e, x, y), (Qk, 0, we), h16)
+        at("sign")
+        for x, y in halves(v0, v1):
+            mm((eps, x - v0, y - v0), ("am", 0, 128), (e, x, y), False, True)
+        for x, y, q in S("sg"):
+            act(("bits%d" % P, x, y), (eps, x - v0, y - v0), F.Sign, bias=("bias", k, k + 1))
+        at("xc")
+        ext(eps, "zc", "bits%d" % P, v0, v1)
+        ts(L("c16_"), (eps, 0, w), 0.5, A.mult, 2047.5, A.add)
+        at("grant")
+        if ch["hf"] == "p":
+            ext(eps, "zh" if (k, ci) in MASKED else "zn", "hb%d" % P, v0, v1, True, False)
+        else:
+            mm((eps, 0, w), ("idh", 0, 128), L("hf"), True, False)
+        mm((eps, 0, w), ("kd" if whole else "kc", 0, 128), ("ones", 0, w), False, False)
+        at("abs")
+        for x, y, q in S("ab"):
+            src = (e, x, y)
+            if got(x, y, "a"):
+                src = (DIST[ci], x - v0, y - v0)
+                for x2, y2 in halves(x, y):
+                    ps, mixed = (DIST[ci], x2 - v0, y2 - v0), got(x2, y2, "v")
+                    if not mixed:
+                        mm(ps, ("idn", 0, 128), (ah, x2, y2), True, False)
+                    mm(ps, ("idp", 0, 128), (e, x2, y2), bool(mixed), not mixed or not got(x2, y2, "a"))
+                    for a, b in got(x2, y2, "a") if mixed else []:
+                        mm((DIST[ci], a - v0, b - v0), ("idn", 0, 128), (ah, a, b), False, True)
+            act(("ae%d" % P, x, y), src, F.Abs, scale=float(2.0 ** -k), bias=-0.5)
+        at("ok")
+        for x, y, q in S("ok"):
+            gtt(("veto%d" % P, x, y), ("clrs", 0, 4096), ("c16_%d" % P, x // 16, y // 16), ("ae%d" % P, x, y), A.is_lt)
+        at("xv")
+        ext(eps, "zv", "veto%d" % P, v0, v1, False)
+        tt(slot("y", 0), (eps, 0, w), par, A.max)
+        at("l3")
+        tt(slot("y", 1), slot("y", 0), ("own", w0, w1), A.min)
+        if last:
+            ts(slot("y", 0, 2), slot("y", 0, 2), 4095, A.bitwise_and)
+            tc(slot("l16_", 1), slot("y", 1))
+            at("names")
+            tc(("pout", w0, w1), slot("y", 0))
+            store(T.yp[:, w0:w1], ("pout", w0, w1))
+            return
+        apart = ch["l3"] or (k + 1, ci) in MASKED
+        if apart:
+            ts(slot("y", 1), slot("y", 1), 4095, A.bitwise_and)
+            tc(slot("l16_", 1), slot("y", 1))
+        at("names")
+        ts(names(k + 1, w0, w1), slot("y", 0), 4095, A.bitwise_and)
+        if ci == 0:
+            share("LL", "an%d" % (k + 1), LW * (k + 1), 32, 4)
+        at("places")
+        places(k + 1, ci, 2 if apart else 1)
+
+    def update(k, ci):
+        ch, P, last = CHUNKS[ci], k % 2, k == RO - 1
+        G["c"], G["k"] = str(ci), k
+        Qk, Qn = "Q%d" % k, "Q%d" % (k + 1)
+        v0, v1 = ch["c"]
+        w0, w = v0 // 16, (v1 - v0) // 16
+        we = M if ci == 0 else W
+        for x, y, q in cut(ch.get("up%d" % k, ch["up"]), v0):
+            a0, a1 = own(x, y)
+            l3 = ("l16_%d" % P, 3 * w0 + w + x // 16, 3 * w0 + w + y // 16)
+            if q == "v":
+                at("upv")
+                gtt((Qn, a0, a1), (Qk, 0, we), l3, ("ah%d" % P, x, y), A.add)
+            else:
+                at("upa")
+                for x2, y2 in halves(x, y):
+                    mm((EPS[ci], x2 - x, y2 - x), ("idh", 0, 128), ("ah%d" % P, x2, y2), True, False)
+                gat("a", ("ub", x, y), (Qk, 0, we), l3)
+                for x2, y2 in halves(x, y):
+                    mm((EPS[ci], x2 - x, y2 - x), ("idp", 0, 128), ("ub", x2, y2), False, True)
+                act((Qn, a0, a1), (EPS[ci], 0, y - x), F.Copy)
+            if last:
+                at("out" + q)
+                if ch["out"] == "a":
+                    act(("yout", x, y), (Qn, a0, a1), F.Identity, scale=float(2.0 ** -RO), bias=-128.0)
+                else:
+                    ts(("yout", x, y), (Qn, a0, a1), 2.0 ** -RO, A.mult, -128.0, A.add, fast=True)
+                store(T.yq[:, x:y], ("yout", x, y))
+        if not last and ci == 0:
+            at("sendq")
+            share(Qn, "aq%d" % (k + 1), 0, B, 2)
 
     for k in range(RO):
-        P = k % 2
-        Qk, Qn, Nk, e = "Q%d" % k, "Q%d" % (k + 1), "nw%d" % k, "e%d" % P
-        for ci, ch in enumerate(CHUNKS):
-            G["c"], G["k"] = str(ci), k
-            v0, v1 = ch["c"]
-            w0, w1 = v0 // 16, v1 // 16
-            w = w1 - w0
-            we = M if ci == 0 else W
-            eps = EPS[ci]
-            L = lambda nm: ("%s%d" % (nm, P), w0, w1)
-            H = lambda j: (eps, 128 * j, 128 * j + w)
-            S = lambda st: cut(ch[st], v0)
-            nf = ("nf%d" % k, w0, w1)
-            ah = ("af%d" if ch["ah"][0] == "a" else "ah%d") % P
-            if ci == 0 and k == 0:
-                for x, y, q in S("hb"):
-                    gtt(("hbh", x, y), ("lw", 0, M // 16), ("hi16", x // 16, y // 16), ("mask", x, y), A.mult)
-                ext(eps, "zh", "hbh", v0, v1)
-            else:
-                for x, y, q in S("hb"):
-                    gat(q, ("hb%d" % P, x, y), (Nk, 0, we), ("n16_%d" % k, x // 16, y // 16))
-                ext(eps, "zn", "hb%d" % P, v0, v1)
-            tc(L("h16_"), H(0))
-            tt(L("dh"), H(0), nf, A.subtract)
-            for x, y, q in S("ah"):
-                if q == "v":
-                    ts((ah, x, y), (Qk,) + own(x, y), -0.5 * 2 ** k, A.add, fast=True)
-                else:
-                    act((ah, x, y), (Qk,) + own(x, y), F.Identity, bias=-0.5 * 2 ** k)
-            for x, y, q in S("e"):
-                h16 = ("h16_%d" % P, x // 16, y // 16)
-                parts = [(bank(), x2, y2) for x2, y2 in halves(x, y)]
-                for ps, x2, y2 in parts:
-                    mm((ps, 0, y2 - x2), ("am2" if q == "v" else "am", 0, 128), (Qk,) + own(x2, y2), True, False)
-                if q == "v":
-                    gtt((e, x, y), (Qk, 0, we), h16, (ah, x, y), A.subtract)
-                else:
-                    gat("a", (e, x, y), (Qk, 0, we), h16)
-                for ps, x2, y2 in parts:
-                    mm((ps, 0, y2 - x2), ("am", 0, 128), (e, x2, y2), False, True)
-                    act(("bits%d" % P, x2, y2), (ps, 0, y2 - x2), F.Sign, bias=("bias" if q == "v" else "biasd", k, k + 1))
-            ext(eps, "zc", "bits%d" % P, v0, v1)
-            ts(L("c16_"), H(0), 0.5, A.mult, 2047.5, A.add)
-            for x, y, q in S("e"):
-                if q == "v":
-                    act(("ae%d" % P, x, y), (e, x, y), F.Abs, scale=float(2.0 ** -k), bias=-0.5)
-                    continue
-                for x2, y2 in halves(x, y):
-                    ps = bank()
-                    mm((ps, 0, y2 - x2), ("idn", 0, 128), (Qk,) + own(x2, y2), True, False)
-                    mm((ps, 0, y2 - x2), ("idp", 0, 128), (e, x2, y2), False, True)
-                    act(("ae%d" % P, x2, y2), (ps, 0, y2 - x2), F.Abs, scale=float(2.0 ** -k))
-            for x, y, q in S("ok"):
-                gtt(("okb%d" % P, x, y), ("clrs", 0, 4096), ("c16_%d" % P, x // 16, y // 16), ("ae%d" % P, x, y), A.is_ge)
-            ext(eps, "z", "okb%d" % P, v0, v1)
-            ts(H(1), H(0), 15.5, A.is_ge)
-            tt(H(2), H(1), L("dn"), A.mult)
-            l3, l4, l16 = ("l34_%d" % P, 2 * w0, w0 + w1), ("l34_%d" % P, w0 + w1, 2 * w1), "l16_%d" % P
-            if k < RO - 1:
-                tt(l4, H(2), ("own", w0, w1), A.add)
-                tc((l16, w0 + w1, 2 * w1), l4)
-                for x, y, q in S("nw"):
-                    o = w0 + w1 + (x - v0) // 16
-                    gat(q, ("nw%d" % (k + 1),) + own(x, y), (Nk, 0, we), (l16, o, o + (y - x) // 16))
-                if ci == 0:
-                    share("nw%d" % (k + 1), "an%d" % (k + 1), own(0, B), B)
-            tt(l3, nf, H(2), A.subtract)
-            tc((l16, 2 * w0, w0 + w1), l3)
-            for x, y, q in S("up"):
-                a0, a1 = own(x, y)
-                o = 2 * w0 + (x - v0) // 16
-                gtt((Qn, a0, a1), (Qk, 0, we), (l16, o, o + (y - x) // 16), (ah, x, y), A.add)
-                if k == RO - 1:
-                    h = (x + y) // 2
-                    act(("yout", x, h), (Qn, a0, a0 + h - x), F.Identity, scale=float(2.0 ** -RO), bias=-128.0)
-                    ts(("yout", h, y), (Qn, a0 + h - x, a1), 2.0 ** -RO, A.mult, -128.0, A.add, fast=True)
-                    store(T.yq[:, x:y], ("yout", x, y))
-            if k < RO - 1 and ci == 0:
-                share(Qn, "aq%d" % (k + 1), own(0, B), B)
-            tt(H(3), H(1), L("dh"), A.mult)
-            tt(("nf%d" % (k + 1), w0, w1), H(3), nf, A.add)
-            if k < RO - 1:
-                tc(("n16_%d" % (k + 1), w0, w1), ("nf%d" % (k + 1), w0, w1))
-                tt(("dn%d" % (1 - P), w0, w1), H(3), L("dn"), A.add)
-            else:
-                store(T.yp[:, w0:w1], ("nf%d" % RO, w0, w1))
+        decide(k, 0)
+        update(k, 0)
+        for stage in (decide, update):
+            for ci in range(1, len(CHUNKS)):
+                stage(k, ci)
     return G, nloc[0]
 
 
@@ -429,7 +590,9 @@ def rank_program(g, core, T, topo):
         return
     G, nloc = build(g, core, T, topo)
     ops = G["ops"]
-    order = schedule(ops)
+    if not ORDER:
+        ORDER.extend(improve(ops, schedule(ops), TRIES, WARM, SEED))
+    order = ORDER
     pos = [0] * len(ops)
     for j, i in enumerate(order):
         pos[i] = j

@@ -1,38 +1,38 @@
 import math
 
 from concourse.bass import DstId, RemoteDMATransfer
-from concourse.mybir import AluOpType, ActivationFunctionType
+from concourse.mybir import AluOpType, ActivationFunctionType, AxisListType
 
 N, V, B, RO = 4, 2048, 512, 5
 M = N * B
 W = M + V - B
 LW = W // 16
+PAD = 256 - LW
 MID = W // 2
 GRANT, VETO = 16384, 32768
 
 CHUNKS = [
-    {'c': (0, 512), 'mk': 'a512', 'ok': 'v512', 'sg': 'a512', 'ab': 'a512', 'l3': True, 'hb0': 'v512', 'hb': 'a512', 'e': 'a512', 'up': 'v512', 'ah': 'v', 'hf': 'v', 'out': 'v', 'e0': 'v384 a128', 'ah0': 'a', 'up4': 'v448 a64'},
-    {'c': (512, 1408), 'mk': 'a896', 'ok': 'v896', 'sg': 'a896', 'ab': 'a896', 'l3': False, 'hb0': 'v896', 'hb': 'v320 a576', 'e': 'a512 v384', 'up': 'v640 a256', 'ah': 'v', 'hf': 'v', 'out': 'a', 'e0': 'a896', 'ah0': 'a', 'up4': 'v608 a288', 'up0': 'v608 a288', 'e4': 'v512 a384'},
-    {'c': (1408, 2048), 'mk': 'a640', 'ok': 'v640', 'sg': 'a640', 'ab': 'a640', 'l3': False, 'hb0': 'v640', 'hb': 'a640', 'e': 'v512 a128', 'up': 'v640', 'ah': 'v', 'hf': 'v', 'out': 'a', 'e0': 'a640', 'ah0': 'a', 'up0': 'v288 a352', 'up4': 'v448 a192', 'hb4': 'v320 a320'},
+    {"c": (0, 512), "hb": "a512", "hb0": "v512", "e": "a512", "e0": "v96 a416", "up": "v512", "ah": "a512", "hf": "p", "l3": True},
+    {"c": (512, 1408), "hb": "v288 a608", "hb0": "v896", "e": "a512 v384", "e0": "a896", "up": "v704 a192", "up0": "v640 a256",
+     "up4": "v384 a512", "ah": "v896", "ah0": "a896", "hf": "v"},
+    {"c": (1408, 2048), "hb": "a640", "hb0": "v640", "e": "v512 a128", "e0": "a640", "up": "v640", "up4": "v320 a320", "ah": "v640",
+     "ah0": "a640", "hf": "p"},
 ]
-MASKED = [(0, 0), (0, 1), (0, 2)]
-FILL = {"NB": "g512 g512 g512 g512", "NI": "v512 v512 g512 g512 g512 g512 g512 g512"}
-EPS = ["ps0", "ps2", "ps6"]
-DIST = ["ps1", "ps4", "ps4"]
+FILL = {"NB": "g512 g512 g512 g512", "NI": "g512 g512 g512 g512 g512 g512 g512 g512"}
+LISTS, SUMS, DIST = ["ps0", "ps2", "ps6"], ["ps0", "ps2", "ps6"], ["ps1", "ps4", "ps4"]
 
 SCRATCH = {}
 _BF, _FH, _F32, _I32, _U16 = "bfloat16", "float16", "float32", "int32", "uint16"
 for _nm, _n, _d in (
-        [(x, 128, _BF) for x in ("am", "idp", "kc", "kd", "ones")] + [(x, 128, _FH) for x in ("amh", "am2", "idn")]
-        + [(x, V, _BF) for x in ("qraw", "yout", "mask", "ub")] + [("clrs", 4096, _BF), ("oh", 16, _BF)]
-        + [(x, 144, _BF) for x in ("zv", "zc")] + [(x, 144, _FH) for x in ("zh", "zn")] + [(x, 128, _FH) for x in ("idh", "hf0", "hf1")]
+        [(x, 128, _BF) for x in ("am", "idp", "kc", "kd", "ones", "rowp")] + [(x, 128, _FH) for x in ("amh", "am2", "idn", "idh")]
+        + [(x, V, _BF) for x in ("qraw", "yout", "ub")] + [("clrs", 4096, _BF), ("oh", 16, _BF), ("mask", V, _BF), ("L0", LW, _F32)]
+        + [(x, 144, _BF) for x in ("zv", "zc")] + [(x, 144, _FH) for x in ("zh", "zn")]
         + [(x, 1, _I32) for x in ("thI", "pI", "pmI")] + [(x, 1, _F32) for x in ("thf", "thd", "pm", "pd")]
         + [(x, 8, _F32) for x in ("bias", "rowg")] + [(x, 16, _F32) for x in ("row", "pw", "p2")]
-        + [(x, 128, _F32) for x in ("own0", "own", "rowp", "pout")]
-        + [("LL", LW * RO, _I32), ("NB", M, _I32), ("NI", 4096, _I32), ("L0", LW, _F32)]
-        + [("Q%d" % k, W, _BF) for k in range(RO + 1)]
+        + [(x, 128, _F32) for x in ("own0", "own", "pout")]
+        + [("LL", PAD + LW * RO, _I32), ("NB", M, _I32), ("NI", 4096, _I32)] + [("Q%d" % k, W, _BF) for k in range(RO + 1)]
         + [("%s%d" % (x, k), V, _BF) for k in range(2) for x in ("bits", "veto", "e", "ae")]
-        + [("%s%d" % (x, k), V, _FH) for k in range(2) for x in ("hb", "ah")]
+        + [("%s%d" % (x, k), V, _FH) for k in range(2) for x in ("hb", "ah")] + [("hf%d" % k, 128, _FH) for k in range(2)]
         + [("%s%d" % (x, k), 128, _U16) for k in range(2) for x in ("h16_", "c16_")]
         + [("y%d" % k, 512, _I32) for k in range(2)] + [("l16_%d" % k, 512, _U16) for k in range(2)]):
     SCRATCH[_nm] = ("sbuf", [128, _n], _d)
@@ -41,11 +41,11 @@ SEMAPHORES = ["sv", "sa", "sp", "sg", "ls"] + ["%s%d" % (x, k) for x in ("an", "
     + ["%s%d" % (x, k) for x in ("ld", "st") for k in range(16)]
 QSEM = {"v": "sv", "a": "sa", "p": "sp", "g": "sg"}
 
-COST = {"fac": 1.25, "gel": 1.56, "pe": 0.45, "wake": 90.0, "same": 30.0, "issue": 700.0, "flight": 1800.0, "col": 2.0, "dma": 2000.0,
-        "act": 90.0, "vec": 5.0}
-LEAD = {}
-PERIOD, PHASE = 125, {}
-TRIES, WARM, SEED = 80000, 400.0, 4
+COST = {"fac": 1.1, "gel": 1.56, "pe": 0.45, "wake": 85.0, "same": 85.0, "issue": 700.0, "first": 1000.0, "flight": 1600.0, "col": 2.0,
+        "dma": 1750.0, "act": 110.0, "vec": 25.0}
+COSTS = [COST, dict(COST, fac=1.06, vec=55.0, wake=65.0, same=25.0, dma=1900.0, first=1600.0),
+         dict(COST, fac=1.05, gel=1.3, wake=130.0, issue=1000.0, flight=2500.0, col=3.5, dma=2300.0), dict(COST, fac=1.4, gel=1.9)]
+TRIES, WARM, SEED = 48000, 350.0, 1
 ORDER = []
 
 
@@ -54,7 +54,7 @@ def cost(o, C):
     if kind == "d":
         return C["dma"] + c[0]
     if kind == "s":
-        return C["issue"]
+        return C["issue"] + c[0] * C["first"]
     if kind == "n":
         return C["flight"] + C["col"] * c[0]
     more = C["act"] if o["q"] == "a" and not c[2] else C["vec"] if o["q"] == "v" else 0.0
@@ -87,12 +87,12 @@ def add(G, q, c, reads, writes, fn, kind="c", sem=None, val=0, deps=()):
                 h[:] = [x for x in h if not ((psum and q == "p") or (x[0] >= c0 and x[1] <= c1 and (
                     not psum or x[2] == i or G["ops"][x[2]]["q"] == q)))]
             h.append((c0, c1, i, kindrw))
-    G["ops"].append({"q": q, "c": c, "fn": fn, "kind": kind, "sem": sem, "val": val, "edges": edges,
-                     "keys": ("%s %s" % (G["c"], G["s"]), "k%d %s" % (G["k"], G["c"]))})
+    G["ops"].append({"q": q, "c": c, "fn": fn, "kind": kind, "sem": sem, "val": val, "edges": edges, "round": G["k"],
+                     "stage": "%s %s" % (G["c"], G["s"])})
     return i
 
 
-def schedule(ops, C=COST, lead=LEAD):
+def schedule(ops, C=COST):
     n = len(ops)
     succ = [[] for _ in range(n)]
     for i, o in enumerate(ops):
@@ -103,18 +103,15 @@ def schedule(ops, C=COST, lead=LEAD):
     way = [0.0] * n
     for i in range(n - 1, -1, -1):
         way[i] = ns[i] + max([way[s] + step(i, s) for s in succ[i]] or [0.0])
-    pri = [w + sum(lead.get(x, 0.0) for x in o["keys"]) for w, o in zip(way, ops)]
-    if PHASE:
-        pri = [-PERIOD * int(o["keys"][1].split()[0][1:]) - PHASE.get(o["keys"][0], 0) for o in ops]
     left = [len(o["edges"]) for o in ops]
     ready = [i for i in range(n) if left[i] == 0]
     busy, start = {}, [0.0] * n
     while ready:
-        i = max(ready, key=lambda x: (pri[x], -x))
+        i = max(ready, key=lambda x: (way[x], -x))
         ready.remove(i)
         t = max([start[d] + ns[d] + step(d, i) for d in ops[i]["edges"]] or [0.0])
         if ops[i]["kind"] != "n":
-            hold = 60.0 if ops[i]["kind"] == "d" else ns[i]
+            hold = ops[i]["c"][1] if ops[i]["kind"] == "d" else ns[i]
             spans = busy.setdefault(ops[i]["q"], [])
             for a, b in spans:
                 if b > t:
@@ -131,28 +128,28 @@ def schedule(ops, C=COST, lead=LEAD):
     return sorted(range(n), key=lambda i: (start[i], i))
 
 
-def improve(ops, order, tries=TRIES, warm=WARM, seed=1, costs=(COST,)):
+def improve(ops, order, tries, warm, seed):
     n, names = len(ops), "vapgsn"
     q = [names.index(o["q"]) for o in ops]
     pred = [set(o["edges"]) for o in ops]
-    ends = set(range(n)) - set().union(*pred)
+    ends = sorted(set(range(n)) - set().union(*pred))
     sets = []
-    for C in costs:
+    for C in COSTS:
         ns = [cost(o, C) for o in ops]
         lag = lambda a, b: C["wake"] if q[a] != q[b] else C["same"] if q[b] != 2 or ops[b]["edges"][a] else 0.0
-        sets.append((ns, [60.0 if o["kind"] == "d" else x for o, x in zip(ops, ns)], [[(d, lag(d, i)) for d in pred[i]] for i in range(n)]))
+        sets.append((ns, [o["c"][1] if o["kind"] == "d" else x for o, x in zip(ops, ns)], [[(d, lag(d, i)) for d in pred[i]] for i in range(n)]))
     state = [seed]
 
     def rnd():
         state[0] = (state[0] * 6364136223846793005 + 1442695040888963407) % 2 ** 64
         return (state[0] >> 11) / 2.0 ** 53
 
-    def run(S, order, j, old):
+    def run(S, order, j, fin, why):
         ns, hold, before = S
         free, last = [0.0] * 6, [-1] * 6
-        fin, why = old[2][:], old[3][:]
-        miss = 5
-        for i in reversed(order[:j]):
+        fin, why, miss = fin[:], why[:], 5
+        for x in range(j - 1, -1, -1):
+            i = order[x]
             if q[i] < 5 and last[q[i]] < 0:
                 last[q[i]], free[q[i]] = i, fin[i] - ns[i] + hold[i]
                 miss -= 1
@@ -161,60 +158,73 @@ def improve(ops, order, tries=TRIES, warm=WARM, seed=1, costs=(COST,)):
         for i in order[j:]:
             k = q[i]
             t, w = free[k], -2 - last[k]
-            for d, lag in before[i]:
-                if fin[d] + lag >= t:
-                    t, w = fin[d] + lag, d
+            for d, gap in before[i]:
+                x = fin[d] + gap
+                if x >= t:
+                    t, w = x, d
             fin[i], why[i] = t + ns[i], w
             if k < 5:
                 free[k], last[k] = t + hold[i], i
-        i = max(ends, key=lambda x: (fin[x], x))
+        i = max(ends, key=lambda x: fin[x])
         return fin[i], i, fin, why
-    now = [run(S, order, 0, (0, 0, [0.0] * n, [0] * n)) for S in sets]
-    total = lambda rs: sum(x[0] for x in rs) / len(rs)
-    best = (total(now), order)
+
+    def move(order, x, y, back):
+        a, b = order.index(x), order.index(y)
+        seg = order[a:b + 1]
+        if back:
+            moved, need = {y}, set(pred[y])
+            for z in reversed(seg[:-1]):
+                if z in need:
+                    moved.add(z)
+                    need |= pred[z]
+        else:
+            moved = {x}
+            for z in seg[1:]:
+                if pred[z] & moved:
+                    moved.add(z)
+        if a >= b or (x in moved and y in moved):
+            return n, order
+        return a, order[:a] + [z for z in seg if (z in moved) == back] + [z for z in seg if (z in moved) != back] + order[b + 1:]
+    place, twin = [], {}
+    for i, o in enumerate(ops):
+        key = (o["round"], o["stage"], q[i], 0)
+        while key in twin:
+            key = key[:3] + (key[3] + 1,)
+        place.append(key)
+        twin[key] = i
+    now = [run(S, order, 0, [0.0] * n, [0] * n) for S in sets]
+    mean = lambda rs: sum(x[0] for x in rs) / len(rs)
+    best = (mean(now), order)
     for it in range(tries):
-        _, i, _, why = now[int(rnd() * len(now))]
+        _, i, _, why = now[it % len(now)]
         held = []
         while why[i] != -1:
             if why[i] < -1:
                 held.append(i)
             i = why[i] if why[i] >= 0 else -2 - why[i]
         i = held[int(rnd() * len(held))]
-        steps = int(-math.log(1.0 - rnd()) / 0.6)
-        a = b = order.index(i)
-        if rnd() < 0.6:
-            steps += 1
-            while a > 0 and steps:
-                a -= 1
-                steps -= q[order[a]] == q[i]
-            seg, moved, need = order[a:b + 1], {i}, set(pred[i])
-            for x in reversed(seg[:-1]):
-                if x in need:
-                    moved.add(x)
-                    need |= pred[x]
-            if seg[0] in moved:
-                continue
-            seg = [x for x in seg if x in moved] + [x for x in seg if x not in moved]
-        else:
-            a = order.index(-2 - why[i])
-            while b < n - 1 and steps:
-                b += 1
-                steps -= q[order[b]] == q[i]
-            seg = order[a:b + 1]
-            moved = {seg[0]}
-            for x in seg[1:]:
-                if pred[x] & moved:
-                    moved.add(x)
-            if i in moved:
-                continue
-            seg = [x for x in seg if x not in moved] + [x for x in seg if x in moved]
-        new = order[:a] + seg + order[b + 1:]
-        then = [run(S, new, a, old) for S, old in zip(sets, now)]
-        d = total(then) - total(now)
+        steps, a = int(-math.log(1.0 - rnd()) / 0.6), order.index(i)
+        back = rnd() < 0.6
+        steps += back
+        while 0 < a < n - 1 and steps:
+            a += -1 if back else 1
+            steps -= q[order[a]] == q[i]
+        x, y = (order[a], i) if back else (-2 - why[i], order[a])
+        a, new = move(order, x, y, back)
+        if new is order:
+            continue
+        if rnd() < 0.8 - 0.6 * it / tries:
+            for d in range(1 - RO, RO):
+                x2, y2 = [twin.get((place[z][0] + d,) + place[z][1:]) for z in (x, y)]
+                if d and x2 is not None and y2 is not None:
+                    b, new = move(new, x2, y2, back)
+                    a = min(a, b)
+        then = [run(S, new, a, old[2], old[3]) for S, old in zip(sets, now)]
+        d = mean(then) - mean(now)
         if d <= 0 or rnd() < math.exp(-d / (warm * (1.0 - it / tries) + 2.0)):
             order, now = new, then
-            if total(now) < best[0]:
-                best = (total(now), order)
+            if mean(now) < best[0]:
+                best = (mean(now), order)
     return best[1]
 
 
@@ -247,8 +257,9 @@ def build(g, core, T, topo):
     def tc(out, in0):
         return add(G, "v", (0, max(64.0, in0[2] - in0[1]), 0), [in0], [out], lambda: g.vector.tensor_copy(X(*out), X(*in0)))
 
-    def ms(out, val):
-        return add(G, "v", (0, max(64.0, out[2] - out[1]), 0), [], [out], lambda: g.vector.memset(X(*out), val))
+    def ms(out, val, fast=False):
+        return add(G, "v", (0, max(64.0, (out[2] - out[1]) * (0.5 if fast else 1.0)), 0), [], [out],
+                   lambda: g.vector.memset(X(*out), val))
 
     def act(out, in0, func, **kw):
         rd = [in0] + [v for v in kw.values() if isinstance(v, tuple)]
@@ -290,7 +301,7 @@ def build(g, core, T, topo):
     def dma(q, sem, reads, writes, dst, src, more=0.0):
         eng = g.sync if q == "s" else g.scalar
         nd[sem] += 1
-        return add(G, q, (more,), reads, writes, lambda: eng.dma_start(dst, src), "d", "%s%d" % (sem, nd[sem] - 1), 16)
+        return add(G, q, (more, 60.0), reads, writes, lambda: eng.dma_start(dst, src), "d", "%s%d" % (sem, nd[sem] - 1), 16)
 
     load = lambda q, out, src, more=0.0: dma(q, "ld", [], [out], X(*out), src, more)
     store = lambda dst, src: dma("s", "st", [src], [], dst, X(*src))
@@ -319,8 +330,8 @@ def build(g, core, T, topo):
                 tr.append(RemoteDMATransfer(dst_ids=ids, dma_engine_mask=sum(1 << e for e in eng), remote_sem=T.sem[sem],
                                             srcs=[X(buf, c0, c1)], dsts=[X(buf, c0, c1)] * len(ids)))
             return g.remote_dma_fused(tr, local_sem=T.sem.ls)
+        i = add(G, "g", (float(nloc[0] == 0),), [(buf, c0, c1)], [], fn, "s")
         nloc[0] += len(efar) + len(enear)
-        i = add(G, "g", (0.0,), [(buf, c0, c1)], [], fn, "s")
         tot = 0
         for c in peers:
             f2 = [x for x in T.cores if topo.chip(x) != topo.chip(c)]
@@ -335,7 +346,9 @@ def build(g, core, T, topo):
 
     def names(k, w0, w1):
         a, b = own(16 * w0, 16 * w1)
-        return ("LL", LW * k + a // 16, LW * k + b // 16)
+        return ("LL", PAD + LW * k + a // 16, PAD + LW * k + b // 16)
+
+    border = lambda k: ("LL", PAD + LW * k, PAD + LW * k + M // 16)
 
     def cut(text, x):
         out = []
@@ -347,24 +360,23 @@ def build(g, core, T, topo):
     def halves(x, y):
         return [(a, min(a + 512, y)) for a in range(x, y, 512)]
 
-    def places(k, ci, first):
+    def slot(nm, k, ci, j, n=1):
         w0, w1 = [x // 16 for x in CHUNKS[ci]["c"]]
-        w, par = w1 - w0, names(k, w0, w1)
-        slot = lambda nm, j, n=1: ("%s%d" % (nm, (k + 1) % 2), 4 * w0 + j * w, 4 * w0 + (j + n) * w)
-        if (k, ci) in MASKED:
-            ts(slot("y", 2), par, 4, A.arith_shift_right)
-            ts(slot("y", 3), par, 15, A.bitwise_and)
-            tc(slot("l16_", 2, 2), slot("y", 2, 2))
-            for x, y, q in cut(CHUNKS[ci]["mk"], 16 * w0):
-                o = slot("l16_", 3)
-                gat(q, ("mask", x, y), ("oh", 0, 16), (o[0], o[1] + x // 16 - w0, o[1] + y // 16 - w0))
-            return
+        return ("%s%d" % (nm, k % 2), 4 * w0 + j * (w1 - w0), 4 * w0 + (j + n) * (w1 - w0))
+
+    def offsets(k, ci, j, x, y):
+        o = slot("l16_", k, ci, j)
+        return (o[0], o[1] + (x - CHUNKS[ci]["c"][0]) // 16, o[1] + (y - CHUNKS[ci]["c"][0]) // 16)
+
+    def places(k, ci, first):
+        par = names(k, CHUNKS[ci]["c"][0] // 16, CHUNKS[ci]["c"][1] // 16)
         if ci == 0:
-            ts(slot("y", 2), par, 128.0625, A.mult, -15.0 / 32, A.add)
+            ts(slot("y", k - 1, ci, 2), par, 128.0625, A.mult, -15.0 / 32, A.add)
         else:
-            ts(slot("y", 2), par, 256.0625, A.mult, (32 if k else 0) - 15.0 / 32 - 112 * 4096, A.add)
-        ts(slot("y", first, 3 - first), slot("y", first, 3 - first), M - 1 if ci == 0 else 4095, A.bitwise_and)
-        tc(slot("l16_", first, 3 - first), slot("y", first, 3 - first))
+            ts(slot("y", k - 1, ci, 2), par, 256.0625, A.mult, PAD - 15.0 / 32 - 112 * 4096, A.add)
+        both = slot("y", k - 1, ci, first, 3 - first)
+        ts(both, both, M - 1 if ci == 0 else 4095, A.bitwise_and)
+        tc(slot("l16_", k - 1, ci, first, 3 - first), both)
 
     at("load")
     load("s", names(0, 0, 32), T.par[:, 0:32])
@@ -385,203 +397,179 @@ def build(g, core, T, topo):
     tc(("pm", 0, 1), ("pmI", 0, 1))
     tt(("pd", 0, 1), ("pI", 0, 1), ("pm", 0, 1), A.subtract)
     ts(("oh", 0, 16), ("row", 0, 16), ("pm", 0, 1), A.is_equal)
-    ms(("zv", 0, 144), 0.0)
+    ms(("zv", 0, 144), 0.0, True)
     ts(("zv", 15, 128, 16), ("rowg", 0, 8), ("pd", 0, 1), A.is_equal, -float(VETO), A.mult)
     ts(("zh", 0, 144), ("zv", 0, 144), -1.0 / VETO, A.mult, fast=True)
-    ts(("zn", 0, 144), ("zh", 0, 144), ("oh", 0, 1), A.mult, fast=True) if False else None
-    ts(("thd", 0, 1), ("pm", 0, 1), 0.0, A.is_equal)
-    ts(("zn", 0, 144), ("zh", 0, 144), ("thd", 0, 1), A.mult, fast=True)
+    ts(("zn", 0, 144), ("zh", 0, 144), ("oh", 0, 1), A.mult, fast=True)
     at("send")
-    share("LL", "an0", 0, 32, 4)
-    a0, a1 = own(0, B)
+    share("LL", "an0", PAD, 32, 4)
     at("sendq")
-    ts(("Q0", a0, a1), ("qraw", 0, B), 128.0, A.add, fast=True)
+    ts(("Q0",) + own(0, B), ("qraw", 0, B), 128.0, A.add, fast=True)
     share("Q0", "aq0", 0, B, 2)
     at("lists")
     for ci, ch in enumerate(CHUNKS):
-        places(0, ci, 2)
-    if (0, 1) in MASKED:
-        at("l0")
-        ts(("L0", 0, LW), ("LL", 0, LW), -float(MID), A.add)
+        v0, v1 = ch["c"]
+        ts(slot("y", -1, ci, 2), names(0, v0 // 16, v1 // 16), 4, A.arith_shift_right)
+        ts(slot("y", -1, ci, 3), names(0, v0 // 16, v1 // 16), 15, A.bitwise_and)
+        tc(slot("l16_", -1, ci, 2, 2), slot("y", -1, ci, 2, 2))
+        gat("a", ("mask", v0, v1), ("oh", 0, 16), slot("l16_", -1, ci, 3))
+    at("l0")
+    ts(("L0", 0, LW), ("LL", PAD, PAD + LW), -float(MID), A.add)
     at("const2")
-    ms(("p2", 0, 1), 1.0)
-    for h in (1, 2, 4, 8):
-        ts(("p2", h, min(2 * h, 12)), ("p2", 0, min(h, 12 - h)), float(2 ** h), A.mult)
-    ms(("p2", 12, 16), 0.0)
-    tt(("pw", 0, 16), ("p2", 0, 16), ("oh", 0, 16), A.mult)
-    for h in (8, 4, 2, 1):
-        tt(("pw", 0, h), ("pw", 0, h), ("pw", h, 2 * h), A.add)
-    ts(("zc", 0, 144), ("zh", 0, 144), ("pw", 0, 1), A.mult, fast=True)
+    ms(("ones", 0, 128), 1.0, True)
+    ms(("pw", 0, 12), 2.0)
+    add(G, "v", (0, 64, 0), [("pw", 0, 12), ("ones", 0, 12)], [("p2", 0, 12)],
+        lambda: g.vector.tensor_tensor_scan(X("p2", 0, 12), X("pw", 0, 12), X("ones", 0, 12), 0.5, A.mult, A.mult))
+    tt(("pw", 0, 12), ("p2", 0, 12), ("oh", 0, 12), A.mult)
+    add(G, "v", (0, 64, 0), [("pw", 0, 12)], [("pw", 12, 13)],
+        lambda: g.vector.tensor_reduce(X("pw", 12, 13), X("pw", 0, 12), AxisListType.X, A.add))
+    ts(("zc", 0, 144), ("zh", 0, 144), ("pw", 12, 13), A.mult, fast=True)
     ts(("own", 0, 128), ("own0", 0, 128), ("pm", 0, 1), A.add)
-    ts(("idp", 0, 128), ("rowp", 0, 128), 0.0, A.is_equal)
-    ts(("idn", 0, 128), ("rowp", 0, 128), 0.0, A.is_equal, -1.0, A.mult)
-    ts(("idh", 0, 128), ("rowp", 0, 128), 0.0, A.is_equal)
-    ms(("kc", 0, 128), (GRANT + MID) / 128.0)
-    ms(("kd", 0, 128), GRANT / 128.0)
-    ms(("ones", 0, 128), 1.0)
+    ts(("idp", 0, 128), ("rowp", 0, 128), 0.0, A.is_equal, fast=True)
+    ts(("idn", 0, 128), ("rowp", 0, 128), 0.0, A.is_equal, -1.0, A.mult, fast=True)
+    ts(("idh", 0, 128), ("rowp", 0, 128), 0.0, A.is_equal, fast=True)
+    ms(("kc", 0, 128), (GRANT + MID) / 128.0, True)
+    ms(("kd", 0, 128), GRANT / 128.0, True)
     mm(("ps7", 0, 2), ("am", 0, 128), ("ones", 0, 2), True, True)
-    tc(("thf", 0, 1), ("thI", 0, 1))
+    ts(("thf", 0, 1), ("thI", 0, 1), 0.5, A.add)
     ts(("thd", 0, 1), ("ps7", 0, 1), 255.5, A.mult, ("thf", 0, 1), A.add)
-    ts(("thd", 0, 1), ("thd", 0, 1), 0.5, A.add, -1.0, A.mult)
-    ts(("bias", 0, 8), ("p2", 0, 8), ("thd", 0, 1), A.mult)
+    ts(("bias", 0, 8), ("p2", 0, 8), ("thd", 0, 1), A.mult, -1.0, A.mult)
     ts(("amh", 0, 128), ("am", 0, 128), 1.0, A.mult, fast=True)
     ts(("am2", 0, 128), ("am", 0, 128), 2.0, A.mult, fast=True)
-    a0, a1 = own(B, V)
     at("q0")
-    ts(("Q0", a0, a1), ("qraw", B, V), 128.0, A.add, fast=True)
+    ts(("Q0",) + own(B, V), ("qraw", B, V), 128.0, A.add, fast=True)
+    at("fillz")
+    if "a" in FILL["NB"] + FILL["NI"]:
+        ms(("ub", 0, 1024), 0.0, True)
     for win in sorted(FILL):
         for x, y, q in cut(FILL[win], 0):
             at("fill" + q)
             if q == "v":
                 ms((win, x, y), 0.0)
+            elif q == "a":
+                act((win, x, y), ("ub", 0, y - x), F.Copy)
             else:
                 io((win, x, y), [[0, y - x]], 0, 0, False)
 
     def decide(k, ci):
         ch, P, last = CHUNKS[ci], k % 2, k == RO - 1
         G["c"], G["k"] = str(ci), k
-        Qk, e = "Q%d" % k, "e%d" % P
+        Qk, e, ah, hb = "Q%d" % k, "e%d" % P, "ah%d" % P, "hb%d" % P
         v0, v1 = ch["c"]
         w0, w1 = v0 // 16, v1 // 16
-        w = w1 - w0
-        we = M if ci == 0 else W
-        eps = EPS[ci]
+        win, lst = (Qk, 0, M if ci == 0 else W), (LISTS[ci], 0, w1 - w0)
         L = lambda nm: ("%s%d" % (nm, P), w0, w1)
         S = lambda st: cut(ch.get(st + str(k), ch[st]), v0)
-        slot = lambda nm, j, n=1, p=P: ("%s%d" % (nm, p), 4 * w0 + j * w, 4 * w0 + (j + n) * w)
-        par, ah = names(k, w0, w1), "ah%d" % P
-        whole = (k, ci) in MASKED and ci == 0
+        whole = k == 0 and ci == 0
         at("lay")
-        if (k, ci) not in MASKED and (ci < 2 or (k, 1) in MASKED):
-            if ci == 0:
-                lay("NB", ("LL", LW * k, LW * k + M // 16))
-            else:
-                lay("NI", ("LL", LW * (k + 1) - 256, LW * (k + 1)) if k else ("LL", 0, 256))
+        if ci == 0 and k:
+            lay("NB", border(k))
+        if ci == 1 and k:
+            lay("NI", ("LL", LW * k, LW * k + 256))
         for x, y, q in S("hb"):
             at("hb" + q)
-            o = slot("l16_", 2, 1, 1 - P)
-            o = (o[0], o[1] + x // 16 - w0, o[1] + y // 16 - w0)
-            if (k, ci) in MASKED:
-                gtt(("hb%d" % P, x, y), ("LL", LW * k, LW * k + M // 16) if whole else ("L0", 0, LW), o, ("mask", x, y), A.mult)
+            if k == 0:
+                gtt((hb, x, y), border(k) if whole else ("L0", 0, LW), offsets(k - 1, ci, 2, x, y), ("mask", x, y), A.mult)
             else:
-                gat(q, ("hb%d" % P, x, y), ("NB", 0, M) if ci == 0 else ("NI", 0, 4096), o, -float(MID))
+                gat(q, (hb, x, y), ("NB", 0, M) if ci == 0 else ("NI", 0, 4096), offsets(k - 1, ci, 2, x, y), -float(MID))
         at("xh")
-        ext(eps, "zh" if (k, ci) in MASKED else "zn", "hb%d" % P, v0, v1)
-        ts(L("h16_"), (eps, 0, w), 0.0 if whole else float(MID), A.add)
+        ext(lst[0], "zn" if k else "zh", hb, v0, v1)
+        ts(L("h16_"), lst, 0.0 if whole else float(MID), A.add)
         at("hf")
         if ch["hf"] == "v":
-            tc(L("hf"), (eps, 0, w))
-        elif ch["hf"] == "a":
-            act(L("hf"), (eps, 0, w), F.Copy)
+            tc(L("hf"), lst)
         at("ah")
-        if ch.get("ah%d" % k, ch["ah"]) == "v":
-            ts((ah, v0, v1), (Qk,) + own(v0, v1), -0.5 * 2 ** k, A.add, fast=True)
-        else:
-            act((ah, v0, v1), (Qk,) + own(v0, v1), F.Identity, bias=-0.5 * 2 ** k)
+        for x, y, q in S("ah"):
+            if q == "v":
+                ts((ah, x, y), (Qk,) + own(x, y), -0.5 * 2 ** k, A.add, fast=True)
+            else:
+                act((ah, x, y), (Qk,) + own(x, y), F.Identity, bias=-0.5 * 2 ** k)
         got = lambda x, y, q: [(max(x, a), min(y, b)) for a, b, c in S("e") if c == q and max(x, a) < min(y, b)]
         at("pre")
         for x, y in halves(v0, v1):
-            mm((eps, x - v0, y - v0), ("amh" if got(x, y, "a") else "am2", 0, 128), (ah, x, y), True, False)
+            mm((SUMS[ci], x - v0, y - v0), ("amh" if got(x, y, "a") else "am2", 0, 128), (ah, x, y), True, False)
             for a, b in got(x, y, "v") if got(x, y, "a") else []:
-                mm((eps, a - v0, b - v0), ("amh", 0, 128), (ah, a, b), False, False)
+                mm((SUMS[ci], a - v0, b - v0), ("amh", 0, 128), (ah, a, b), False, False)
         for x, y, q in S("e"):
-            h16 = ("h16_%d" % P, x // 16, y // 16)
             at("e" + q)
             if q == "v":
-                gtt((e, x, y), (Qk, 0, we), h16, (ah, x, y), A.subtract)
+                gtt((e, x, y), win, ("h16_%d" % P, x // 16, y // 16), (ah, x, y), A.subtract)
             else:
-                gat("a", (e, x, y), (Qk, 0, we), h16)
+                gat(q, (e, x, y), win, ("h16_%d" % P, x // 16, y // 16))
         at("sign")
         for x, y in halves(v0, v1):
-            mm((eps, x - v0, y - v0), ("am", 0, 128), (e, x, y), False, True)
-        for x, y, q in S("sg"):
-            act(("bits%d" % P, x, y), (eps, x - v0, y - v0), F.Sign, bias=("bias", k, k + 1))
+            mm((SUMS[ci], x - v0, y - v0), ("am", 0, 128), (e, x, y), False, True)
+        act(("bits%d" % P, v0, v1), (SUMS[ci], 0, v1 - v0), F.Sign, bias=("bias", k, k + 1))
         at("xc")
-        ext(eps, "zc", "bits%d" % P, v0, v1)
-        ts(L("c16_"), (eps, 0, w), 0.5, A.mult, 2047.5, A.add)
-        at("grant")
-        if ch["hf"] == "p":
-            ext(eps, "zh" if (k, ci) in MASKED else "zn", "hb%d" % P, v0, v1, True, False)
-        else:
-            mm((eps, 0, w), ("idh", 0, 128), L("hf"), True, False)
-        mm((eps, 0, w), ("kd" if whole else "kc", 0, 128), ("ones", 0, w), False, False)
+        ext(lst[0], "zc", "bits%d" % P, v0, v1)
+        ts(L("c16_"), lst, 0.5, A.mult, 2047.5, A.add)
         at("abs")
-        for x, y, q in S("ab"):
-            src = (e, x, y)
-            if got(x, y, "a"):
-                src = (DIST[ci], x - v0, y - v0)
-                for x2, y2 in halves(x, y):
-                    ps, mixed = (DIST[ci], x2 - v0, y2 - v0), got(x2, y2, "v")
-                    if not mixed:
-                        mm(ps, ("idn", 0, 128), (ah, x2, y2), True, False)
-                    mm(ps, ("idp", 0, 128), (e, x2, y2), bool(mixed), not mixed or not got(x2, y2, "a"))
-                    for a, b in got(x2, y2, "a") if mixed else []:
-                        mm((DIST[ci], a - v0, b - v0), ("idn", 0, 128), (ah, a, b), False, True)
-            act(("ae%d" % P, x, y), src, F.Abs, scale=float(2.0 ** -k), bias=-0.5)
+        for x, y in halves(v0, v1):
+            ps, mixed = (DIST[ci], x - v0, y - v0), got(x, y, "v")
+            if not mixed:
+                mm(ps, ("idn", 0, 128), (ah, x, y), True, False)
+            mm(ps, ("idp", 0, 128), (e, x, y), bool(mixed), not mixed or not got(x, y, "a"))
+            for a, b in got(x, y, "a") if mixed else []:
+                mm((DIST[ci], a - v0, b - v0), ("idn", 0, 128), (ah, a, b), False, True)
+        act(("ae%d" % P, v0, v1), (DIST[ci], 0, v1 - v0), F.Abs, scale=float(2.0 ** -k), bias=-0.5)
         at("ok")
-        for x, y, q in S("ok"):
-            gtt(("veto%d" % P, x, y), ("clrs", 0, 4096), ("c16_%d" % P, x // 16, y // 16), ("ae%d" % P, x, y), A.is_lt)
+        gtt(("veto%d" % P, v0, v1), ("clrs", 0, 4096), L("c16_"), ("ae%d" % P, v0, v1), A.is_lt)
+        at("grant")
+        mm(lst, ("kd" if whole else "kc", 0, 128), ("ones", 0, w1 - w0), True, False)
+        if ch["hf"] == "p":
+            ext(lst[0], "zn" if k else "zh", hb, v0, v1, False, False)
+        else:
+            mm(lst, ("idh", 0, 128), L("hf"), False, False)
         at("xv")
-        ext(eps, "zv", "veto%d" % P, v0, v1, False)
-        tt(slot("y", 0), (eps, 0, w), par, A.max)
+        ext(lst[0], "zv", "veto%d" % P, v0, v1, False)
+        tt(slot("y", k, ci, 0), lst, names(k, w0, w1), A.max)
         at("l3")
-        tt(slot("y", 1), slot("y", 0), ("own", w0, w1), A.min)
+        tt(slot("y", k, ci, 1), slot("y", k, ci, 0), ("own", w0, w1), A.min)
         if last:
-            ts(slot("y", 0, 2), slot("y", 0, 2), 4095, A.bitwise_and)
-            tc(slot("l16_", 1), slot("y", 1))
+            ts(slot("y", k, ci, 0, 2), slot("y", k, ci, 0, 2), 4095, A.bitwise_and)
+            tc(slot("l16_", k, ci, 1), slot("y", k, ci, 1))
             at("names")
-            tc(("pout", w0, w1), slot("y", 0))
+            tc(("pout", w0, w1), slot("y", k, ci, 0))
             store(T.yp[:, w0:w1], ("pout", w0, w1))
             return
-        apart = ch["l3"] or (k + 1, ci) in MASKED
-        if apart:
-            ts(slot("y", 1), slot("y", 1), 4095, A.bitwise_and)
-            tc(slot("l16_", 1), slot("y", 1))
+        if ch.get("l3"):
+            ts(slot("y", k, ci, 1), slot("y", k, ci, 1), 4095, A.bitwise_and)
+            tc(slot("l16_", k, ci, 1), slot("y", k, ci, 1))
         at("names")
-        ts(names(k + 1, w0, w1), slot("y", 0), 4095, A.bitwise_and)
+        ts(names(k + 1, w0, w1), slot("y", k, ci, 0), 4095, A.bitwise_and)
         if ci == 0:
-            share("LL", "an%d" % (k + 1), LW * (k + 1), 32, 4)
+            share("LL", "an%d" % (k + 1), PAD + LW * (k + 1), 32, 4)
         at("places")
-        places(k + 1, ci, 2 if apart else 1)
+        places(k + 1, ci, 2 if ch.get("l3") else 1)
 
     def update(k, ci):
-        ch, P, last = CHUNKS[ci], k % 2, k == RO - 1
+        ch, last = CHUNKS[ci], k == RO - 1
         G["c"], G["k"] = str(ci), k
         Qk, Qn = "Q%d" % k, "Q%d" % (k + 1)
-        v0, v1 = ch["c"]
-        w0, w = v0 // 16, (v1 - v0) // 16
-        we = M if ci == 0 else W
-        for x, y, q in cut(ch.get("up%d" % k, ch["up"]), v0):
-            a0, a1 = own(x, y)
-            l3 = ("l16_%d" % P, 3 * w0 + w + x // 16, 3 * w0 + w + y // 16)
+        win = (Qk, 0, M if ci == 0 else W)
+        for x, y, q in cut(ch.get("up%d" % k, ch["up"]), ch["c"][0]):
+            new, ps = (Qn,) + own(x, y), (SUMS[ci], 0, y - x)
+            at("up" + q)
             if q == "v":
-                at("upv")
-                gtt((Qn, a0, a1), (Qk, 0, we), l3, ("ah%d" % P, x, y), A.add)
+                gtt(new, win, offsets(k, ci, 1, x, y), ("ah%d" % (k % 2), x, y), A.add)
             else:
-                at("upa")
-                for x2, y2 in halves(x, y):
-                    mm((EPS[ci], x2 - x, y2 - x), ("idh", 0, 128), ("ah%d" % P, x2, y2), True, False)
-                gat("a", ("ub", x, y), (Qk, 0, we), l3)
-                for x2, y2 in halves(x, y):
-                    mm((EPS[ci], x2 - x, y2 - x), ("idp", 0, 128), ("ub", x2, y2), False, True)
-                act((Qn, a0, a1), (EPS[ci], 0, y - x), F.Copy)
+                mm(ps, ("idp", 0, 128), (Qk,) + own(x, y), True, False)
+                gat(q, ("ub", x, y), win, offsets(k, ci, 1, x, y))
+                mm(ps, ("idp", 0, 128), ("ub", x, y), False, True)
+                act(new, ps, F.Identity, bias=-0.5 * 2 ** k)
             if last:
                 at("out" + q)
-                if ch["out"] == "a":
-                    act(("yout", x, y), (Qn, a0, a1), F.Identity, scale=float(2.0 ** -RO), bias=-128.0)
-                else:
-                    ts(("yout", x, y), (Qn, a0, a1), 2.0 ** -RO, A.mult, -128.0, A.add, fast=True)
+                ts(("yout", x, y), new, 2.0 ** -RO, A.mult, -128.0, A.add, fast=True)
                 store(T.yq[:, x:y], ("yout", x, y))
         if not last and ci == 0:
             at("sendq")
             share(Qn, "aq%d" % (k + 1), 0, B, 2)
 
     for k in range(RO):
-        decide(k, 0)
-        update(k, 0)
-        for stage in (decide, update):
-            for ci in range(1, len(CHUNKS)):
-                stage(k, ci)
+        for cis in ([0], range(1, len(CHUNKS))):
+            for stage in (decide, update):
+                for ci in cis:
+                    stage(k, ci)
     return G, nloc[0]
 
 
@@ -591,7 +579,7 @@ def rank_program(g, core, T, topo):
     G, nloc = build(g, core, T, topo)
     ops = G["ops"]
     if not ORDER:
-        ORDER.extend(improve(ops, schedule(ops), TRIES, WARM, SEED))
+        ORDER.extend(sorted(improve(ops, schedule(ops), TRIES, WARM, SEED), key=lambda i: i if ops[i]["stage"] == "i load" else len(ops)))
     order = ORDER
     pos = [0] * len(ops)
     for j, i in enumerate(order):

import math

from concourse.bass import DstId, RemoteDMATransfer
from concourse.mybir import AluOpType, ActivationFunctionType, AxisListType

N, V, B, RO = 4, 2048, 512, 5
M = N * B
W = M + V - B
LW = W // 16
PAD = 256 - LW
MID = W // 2
GRANT, VETO = 16384, 32768

CHUNKS = [
    {"c": (0, 512), "hb": "a512", "hb0": "v512", "e": "a512", "e0": "v96 a416", "up": "v512", "ah": "a512", "hf": "p", "l3": True},
    {"c": (512, 1408), "hb": "v288 a608", "hb0": "v896", "e": "a512 v384", "e0": "a896", "up": "v704 a192", "up0": "v640 a256",
     "up4": "v384 a512", "ah": "v896", "ah0": "a896", "hf": "v"},
    {"c": (1408, 2048), "hb": "a640", "hb0": "v640", "e": "v512 a128", "e0": "a640", "up": "v640", "up4": "v320 a320", "ah": "v640",
     "ah0": "a640", "hf": "p"},
]
FILL = {"NB": "g512 g512 g512 g512", "NI": "g512 g512 g512 g512 g512 g512 g512 g512"}
LISTS, SUMS, DIST = ["ps0", "ps2", "ps6"], ["ps0", "ps2", "ps6"], ["ps1", "ps4", "ps4"]

SCRATCH = {}
_BF, _FH, _F32, _I32, _U16 = "bfloat16", "float16", "float32", "int32", "uint16"
for _nm, _n, _d in (
        [(x, 128, _BF) for x in ("am", "idp", "kc", "kd", "ones", "rowp")] + [(x, 128, _FH) for x in ("amh", "am2", "idn", "idh")]
        + [(x, V, _BF) for x in ("qraw", "yout", "ub")] + [("clrs", 4096, _BF), ("oh", 16, _BF), ("mask", V, _BF), ("L0", LW, _F32)]
        + [(x, 144, _BF) for x in ("zv", "zc")] + [(x, 144, _FH) for x in ("zh", "zn")]
        + [(x, 1, _I32) for x in ("thI", "pI", "pmI")] + [(x, 1, _F32) for x in ("thf", "thd", "pm", "pd")]
        + [(x, 8, _F32) for x in ("bias", "rowg")] + [(x, 16, _F32) for x in ("row", "pw", "p2")]
        + [(x, 128, _F32) for x in ("own0", "own", "pout")]
        + [("LL", PAD + LW * RO, _I32), ("NB", M, _I32), ("NI", 4096, _I32)] + [("Q%d" % k, W, _BF) for k in range(RO + 1)]
        + [("%s%d" % (x, k), V, _BF) for k in range(2) for x in ("bits", "veto", "e", "ae")]
        + [("%s%d" % (x, k), V, _FH) for k in range(2) for x in ("hb", "ah")] + [("hf%d" % k, 128, _FH) for k in range(2)]
        + [("%s%d" % (x, k), 128, _U16) for k in range(2) for x in ("h16_", "c16_")]
        + [("y%d" % k, 512, _I32) for k in range(2)] + [("l16_%d" % k, 512, _U16) for k in range(2)]):
    SCRATCH[_nm] = ("sbuf", [128, _n], _d)
SCRATCH["ps"] = ("psum", [128, 4096], "float32")
SEMAPHORES = ["sv", "sa", "sp", "sg", "ls"] + ["%s%d" % (x, k) for x in ("an", "aq") for k in range(RO)] \
    + ["%s%d" % (x, k) for x in ("ld", "st") for k in range(16)]
QSEM = {"v": "sv", "a": "sa", "p": "sp", "g": "sg"}

COST = {"fac": 1.1, "gel": 1.56, "pe": 0.45, "wake": 85.0, "same": 85.0, "issue": 700.0, "first": 1000.0, "flight": 1600.0, "col": 2.0,
        "dma": 1750.0, "act": 110.0, "vec": 25.0}
COSTS = [COST, dict(COST, fac=1.06, vec=55.0, wake=65.0, same=25.0, dma=1900.0, first=1600.0),
         dict(COST, fac=1.05, gel=1.3, wake=130.0, issue=1000.0, flight=2500.0, col=3.5, dma=2300.0), dict(COST, fac=1.4, gel=1.9)]
TRIES, WARM, SEED = 48000, 350.0, 1
ORDER = []


def cost(o, C):
    kind, c = o["kind"], o["c"]
    if kind == "d":
        return C["dma"] + c[0]
    if kind == "s":
        return C["issue"] + c[0] * C["first"]
    if kind == "n":
        return C["flight"] + C["col"] * c[0]
    more = C["act"] if o["q"] == "a" and not c[2] else C["vec"] if o["q"] == "v" else 0.0
    return more + C["fac"] * (C["pe"] * c[1] if o["q"] == "p" else c[0] + 0.83 * (c[1] + C["gel"] * c[2]))


def add(G, q, c, reads, writes, fn, kind="c", sem=None, val=0, deps=()):
    i = len(G["ops"])
    edges = {d: True for d in deps}
    banks = lambda regs: [y for nm, a, b in regs for y in (
        [("ps%d" % (int(nm[2:]) + j), max(a - 512 * j, 0), min(b - 512 * j, 512)) for j in range(a // 512, -(-b // 512))]
        if nm[:2] == "ps" else [(nm, a, b)])]
    reads, writes = banks(reads), banks(writes)
    for kindrw, regs in ((0, reads), (1, writes)):
        for (nm, c0, c1) in regs:
            psum = nm[:2] == "ps"
            for (a0, a1, o, w) in G["hist"].setdefault(nm, []):
                other = psum and G["ops"][o]["q"] != q
                if not other and (a0 >= c1 or c0 >= a1):
                    continue
                if w and not kindrw:
                    edges[o] = True
                elif kindrw or other:
                    edges.setdefault(o, False)
    for kindrw, regs in ((0, reads), (1, writes)):
        for (nm, c0, c1) in regs:
            h = G["hist"][nm]
            psum = nm[:2] == "ps"
            if kindrw:
                h[:] = [x for x in h if not ((psum and q == "p") or (x[0] >= c0 and x[1] <= c1 and (
                    not psum or x[2] == i or G["ops"][x[2]]["q"] == q)))]
            h.append((c0, c1, i, kindrw))
    G["ops"].append({"q": q, "c": c, "fn": fn, "kind": kind, "sem": sem, "val": val, "edges": edges, "round": G["k"],
                     "stage": "%s %s" % (G["c"], G["s"])})
    return i


def schedule(ops, C=COST):
    n = len(ops)
    succ = [[] for _ in range(n)]
    for i, o in enumerate(ops):
        for d in o["edges"]:
            succ[d].append(i)
    step = lambda a, b: C["wake"] if ops[a]["q"] != ops[b]["q"] else C["same"]
    ns = [cost(o, C) for o in ops]
    way = [0.0] * n
    for i in range(n - 1, -1, -1):
        way[i] = ns[i] + max([way[s] + step(i, s) for s in succ[i]] or [0.0])
    left = [len(o["edges"]) for o in ops]
    ready = [i for i in range(n) if left[i] == 0]
    busy, start = {}, [0.0] * n
    while ready:
        i = max(ready, key=lambda x: (way[x], -x))
        ready.remove(i)
        t = max([start[d] + ns[d] + step(d, i) for d in ops[i]["edges"]] or [0.0])
        if ops[i]["kind"] != "n":
            hold = ops[i]["c"][1] if ops[i]["kind"] == "d" else ns[i]
            spans = busy.setdefault(ops[i]["q"], [])
            for a, b in spans:
                if b > t:
                    if t + hold <= a:
                        break
                    t = b
            spans.append((t, t + hold))
            spans.sort()
        start[i] = t
        for x in succ[i]:
            left[x] -= 1
            if left[x] == 0:
                ready.append(x)
    return sorted(range(n), key=lambda i: (start[i], i))


def improve(ops, order, tries, warm, seed):
    n, names = len(ops), "vapgsn"
    q = [names.index(o["q"]) for o in ops]
    pred = [set(o["edges"]) for o in ops]
    ends = sorted(set(range(n)) - set().union(*pred))
    sets = []
    for C in COSTS:
        ns = [cost(o, C) for o in ops]
        lag = lambda a, b: C["wake"] if q[a] != q[b] else C["same"] if q[b] != 2 or ops[b]["edges"][a] else 0.0
        sets.append((ns, [o["c"][1] if o["kind"] == "d" else x for o, x in zip(ops, ns)], [[(d, lag(d, i)) for d in pred[i]] for i in range(n)]))
    state = [seed]

    def rnd():
        state[0] = (state[0] * 6364136223846793005 + 1442695040888963407) % 2 ** 64
        return (state[0] >> 11) / 2.0 ** 53

    def run(S, order, j, fin, why):
        ns, hold, before = S
        free, last = [0.0] * 6, [-1] * 6
        fin, why, miss = fin[:], why[:], 5
        for x in range(j - 1, -1, -1):
            i = order[x]
            if q[i] < 5 and last[q[i]] < 0:
                last[q[i]], free[q[i]] = i, fin[i] - ns[i] + hold[i]
                miss -= 1
                if not miss:
                    break
        for i in order[j:]:
            k = q[i]
            t, w = free[k], -2 - last[k]
            for d, gap in before[i]:
                x = fin[d] + gap
                if x >= t:
                    t, w = x, d
            fin[i], why[i] = t + ns[i], w
            if k < 5:
                free[k], last[k] = t + hold[i], i
        i = max(ends, key=lambda x: fin[x])
        return fin[i], i, fin, why

    def move(order, x, y, back):
        a, b = order.index(x), order.index(y)
        seg = order[a:b + 1]
        if back:
            moved, need = {y}, set(pred[y])
            for z in reversed(seg[:-1]):
                if z in need:
                    moved.add(z)
                    need |= pred[z]
        else:
            moved = {x}
            for z in seg[1:]:
                if pred[z] & moved:
                    moved.add(z)
        if a >= b or (x in moved and y in moved):
            return n, order
        return a, order[:a] + [z for z in seg if (z in moved) == back] + [z for z in seg if (z in moved) != back] + order[b + 1:]
    place, twin = [], {}
    for i, o in enumerate(ops):
        key = (o["round"], o["stage"], q[i], 0)
        while key in twin:
            key = key[:3] + (key[3] + 1,)
        place.append(key)
        twin[key] = i
    now = [run(S, order, 0, [0.0] * n, [0] * n) for S in sets]
    mean = lambda rs: sum(x[0] for x in rs) / len(rs)
    best = (mean(now), order)
    for it in range(tries):
        _, i, _, why = now[it % len(now)]
        held = []
        while why[i] != -1:
            if why[i] < -1:
                held.append(i)
            i = why[i] if why[i] >= 0 else -2 - why[i]
        i = held[int(rnd() * len(held))]
        steps, a = int(-math.log(1.0 - rnd()) / 0.6), order.index(i)
        back = rnd() < 0.6
        steps += back
        while 0 < a < n - 1 and steps:
            a += -1 if back else 1
            steps -= q[order[a]] == q[i]
        x, y = (order[a], i) if back else (-2 - why[i], order[a])
        a, new = move(order, x, y, back)
        if new is order:
            continue
        if rnd() < 0.8 - 0.6 * it / tries:
            for d in range(1 - RO, RO):
                x2, y2 = [twin.get((place[z][0] + d,) + place[z][1:]) for z in (x, y)]
                if d and x2 is not None and y2 is not None:
                    b, new = move(new, x2, y2, back)
                    a = min(a, b)
        then = [run(S, new, a, old[2], old[3]) for S, old in zip(sets, now)]
        d = mean(then) - mean(now)
        if d <= 0 or rnd() < math.exp(-d / (warm * (1.0 - it / tries) + 2.0)):
            order, now = new, then
            if mean(now) < best[0]:
                best = (mean(now), order)
    return best[1]


def build(g, core, T, topo):
    A, F = AluOpType, ActivationFunctionType
    r = T.rank_of(core)
    G = {"ops": [], "hist": {}, "c": "i", "k": -1, "s": ""}

    def X(nm, a, b, s=1):
        if nm[:2] == "ps":
            return T.ps[:, 512 * int(nm[2:]) + a:512 * int(nm[2:]) + b]
        return T[nm][:, a:b] if s == 1 else T[nm][:, a:b:s]
    Y = lambda s: X(*s) if isinstance(s, tuple) else s

    def at(stage):
        G["s"] = stage

    def ts(out, in0, s1, op0, s2=None, op1=None, fast=False):
        def fn():
            if op1 is None:
                return g.vector.tensor_scalar(X(*out), X(*in0), Y(s1), None, op0)
            return g.vector.tensor_scalar(X(*out), X(*in0), Y(s1), Y(s2), op0, op1)
        rd = [in0] + [s for s in (s1, s2) if isinstance(s, tuple)]
        return add(G, "v", (0, max(64.0, (in0[2] - in0[1]) * (0.5 if fast else 1.0)), 0), rd, [out[:3]], fn)

    def tt(out, in0, in1, op):
        cyc = max(64.0, (in0[2] - in0[1]) * (1.0 if "ps" in (in0[0][:2], in1[0][:2]) else 2.0))
        return add(G, "v", (0, cyc, 0), [in0, in1], [out], lambda: g.vector.tensor_tensor(X(*out), X(*in0), X(*in1), op))

    def tc(out, in0):
        return add(G, "v", (0, max(64.0, in0[2] - in0[1]), 0), [in0], [out], lambda: g.vector.tensor_copy(X(*out), X(*in0)))

    def ms(out, val, fast=False):
        return add(G, "v", (0, max(64.0, (out[2] - out[1]) * (0.5 if fast else 1.0)), 0), [], [out],
                   lambda: g.vector.memset(X(*out), val))

    def act(out, in0, func, **kw):
        rd = [in0] + [v for v in kw.values() if isinstance(v, tuple)]
        return add(G, "a", (40, max(64.0, in0[2] - in0[1]), 0), rd, [out],
                   lambda: g.scalar.activation(X(*out), X(*in0), func, **{nm: Y(v) for nm, v in kw.items()}))

    def gat(q, out, win, off, plus=0.0):
        def fn():
            w = X(*win).indirect(X(*off))
            if q == "v":
                return g.vector.tensor_scalar(X(*out), w, plus, None, A.add)
            return g.scalar.activation(X(*out), w, F.Identity, bias=plus)
        return add(G, q, (50 if q == "v" else 65, 0, out[2] - out[1]), [win, off], [out], fn)

    def gtt(out, win, off, in1, op):
        return add(G, "v", (50, 0, out[2] - out[1]), [win, off, in1], [out],
                   lambda: g.vector.tensor_tensor(X(*out), X(*win).indirect(X(*off)), X(*in1), op))

    def mm(outs, lhs, rhs, start, stop):
        return add(G, "p", (0, max(64, rhs[2] - rhs[1]), 0), [lhs, rhs], [outs],
                   lambda: g.tensor.matmul(X(*outs), X(*lhs), X(*rhs), start, stop))

    def ext(ps, zname, src, v0, v1, start=True, stop=True):
        w = (v1 - v0) // 16

        def fn():
            for i in range(16):
                ins = g.tensor.matmul(X(ps, 0, w), T[zname][:, 15 - i:143 - i], T[src][:, v0 + i:v1:16], start and i == 0,
                                      stop and i == 15)
            return ins
        return add(G, "p", (0, 16 * max(64, w), 0), [(zname, 0, 144), (src, v0, v1)], [(ps, 0, w)], fn)

    def io(out, pattern, base, cm, flag=True):
        kw = {"allow_small_or_imprecise_dtypes": True} if flag else {}
        return add(G, "g", (130, 2 * (out[2] - out[1]), 0), [], [out], lambda: g.iota(X(*out), pattern, base, cm, **kw))

    nd = {"ld": 0, "st": 0}

    def dma(q, sem, reads, writes, dst, src, more=0.0):
        eng = g.sync if q == "s" else g.scalar
        nd[sem] += 1
        return add(G, q, (more, 60.0), reads, writes, lambda: eng.dma_start(dst, src), "d", "%s%d" % (sem, nd[sem] - 1), 16)

    load = lambda q, out, src, more=0.0: dma(q, "ld", [], [out], X(*out), src, more)
    store = lambda dst, src: dma("s", "st", [src], [], dst, X(*src))

    def lay(win, src):
        n = 16 * (src[2] - src[1])
        return dma("s", "ld", [src], [(win, 0, n)], T[win][0:128:16, 0:n], X(*src))

    peers = [c for c in T.cores if c != core]
    near = [c for c in peers if topo.chip(c) == topo.chip(core)]
    far = [c for c in peers if topo.chip(c) != topo.chip(core)]
    efar = [e for e in topo.engines(core, far[0]) if all(e in topo.engines(core, c) for c in far)]
    enear = [e for e in topo.engines(core, near[0]) if e not in efar]
    nloc = [0]

    def share(buf, sem, base, step, size):
        c0, c1 = base + r * step, base + (r + 1) * step

        def fn():
            tr = []
            for dsts, eng in ((far, efar), (near, enear)):
                ids = []
                for c in dsts:
                    rid, pid, se = topo.addr(c)
                    ids.append(DstId(rid=rid, pnc=pid))
                tr.append(RemoteDMATransfer(dst_ids=ids, dma_engine_mask=sum(1 << e for e in eng), remote_sem=T.sem[sem],
                                            srcs=[X(buf, c0, c1)], dsts=[X(buf, c0, c1)] * len(ids)))
            return g.remote_dma_fused(tr, local_sem=T.sem.ls)
        i = add(G, "g", (float(nloc[0] == 0),), [(buf, c0, c1)], [], fn, "s")
        nloc[0] += len(efar) + len(enear)
        tot = 0
        for c in peers:
            f2 = [x for x in T.cores if topo.chip(x) != topo.chip(c)]
            e2 = topo.engines(c, f2[0])
            tot += len(e2) if topo.chip(c) != topo.chip(core) else len([e for e in topo.engines(c, core) if e not in e2])
        wr = [(buf, a, b) for (a, b) in ((base, c0), (c1, base + N * step)) if b > a]
        add(G, "n", (step * size // 2,), [], wr, None, "n", sem, tot, deps=[i])

    def own(v0, v1):
        o = r * B if v1 <= B else M - B
        return (v0 + o, v1 + o)

    def names(k, w0, w1):
        a, b = own(16 * w0, 16 * w1)
        return ("LL", PAD + LW * k + a // 16, PAD + LW * k + b // 16)

    border = lambda k: ("LL", PAD + LW * k, PAD + LW * k + M // 16)

    def cut(text, x):
        out = []
        for t in text.split():
            out.append((x, x + int(t[1:]), t[0]))
            x = out[-1][1]
        return out

    def halves(x, y):
        return [(a, min(a + 512, y)) for a in range(x, y, 512)]

    def slot(nm, k, ci, j, n=1):
        w0, w1 = [x // 16 for x in CHUNKS[ci]["c"]]
        return ("%s%d" % (nm, k % 2), 4 * w0 + j * (w1 - w0), 4 * w0 + (j + n) * (w1 - w0))

    def offsets(k, ci, j, x, y):
        o = slot("l16_", k, ci, j)
        return (o[0], o[1] + (x - CHUNKS[ci]["c"][0]) // 16, o[1] + (y - CHUNKS[ci]["c"][0]) // 16)

    def places(k, ci, first):
        par = names(k, CHUNKS[ci]["c"][0] // 16, CHUNKS[ci]["c"][1] // 16)
        if ci == 0:
            ts(slot("y", k - 1, ci, 2), par, 128.0625, A.mult, -15.0 / 32, A.add)
        else:
            ts(slot("y", k - 1, ci, 2), par, 256.0625, A.mult, PAD - 15.0 / 32 - 112 * 4096, A.add)
        both = slot("y", k - 1, ci, first, 3 - first)
        ts(both, both, M - 1 if ci == 0 else 4095, A.bitwise_and)
        tc(slot("l16_", k - 1, ci, first, 3 - first), both)

    at("load")
    load("s", names(0, 0, 32), T.par[:, 0:32])
    load("a", ("qraw", 0, B), T.q[:, 0:B])
    load("s", names(0, 32, 128), T.par[:, 32:128])
    load("s", ("am", 0, 128), T.amat[:, :])
    load("s", ("thI", 0, 1), T.th[:, :])
    load("s", ("qraw", B, V), T.q[:, B:V], 1000.0)
    load("s", ("clrs", 0, 4096), T.clr[:, :], 3000.0)
    at("const")
    io(("pI", 0, 1), [[0, 1]], 0, 1, False)
    io(("rowg", 0, 8), [[16, 8]], 0, 0)
    io(("row", 0, 16), [[1, 16]], 0, 0)
    io(("own0", 0, 32), [[16, 32]], 4096 + r * B, 0)
    io(("own0", 32, 128), [[16, 96]], 4096 + M, 0)
    io(("rowp", 0, 128), [[1, 128]], 0, -1)
    ts(("pmI", 0, 1), ("pI", 0, 1), 15, A.bitwise_and)
    tc(("pm", 0, 1), ("pmI", 0, 1))
    tt(("pd", 0, 1), ("pI", 0, 1), ("pm", 0, 1), A.subtract)
    ts(("oh", 0, 16), ("row", 0, 16), ("pm", 0, 1), A.is_equal)
    ms(("zv", 0, 144), 0.0, True)
    ts(("zv", 15, 128, 16), ("rowg", 0, 8), ("pd", 0, 1), A.is_equal, -float(VETO), A.mult)
    ts(("zh", 0, 144), ("zv", 0, 144), -1.0 / VETO, A.mult, fast=True)
    ts(("zn", 0, 144), ("zh", 0, 144), ("oh", 0, 1), A.mult, fast=True)
    at("send")
    share("LL", "an0", PAD, 32, 4)
    at("sendq")
    ts(("Q0",) + own(0, B), ("qraw", 0, B), 128.0, A.add, fast=True)
    share("Q0", "aq0", 0, B, 2)
    at("lists")
    for ci, ch in enumerate(CHUNKS):
        v0, v1 = ch["c"]
        ts(slot("y", -1, ci, 2), names(0, v0 // 16, v1 // 16), 4, A.arith_shift_right)
        ts(slot("y", -1, ci, 3), names(0, v0 // 16, v1 // 16), 15, A.bitwise_and)
        tc(slot("l16_", -1, ci, 2, 2), slot("y", -1, ci, 2, 2))
        gat("a", ("mask", v0, v1), ("oh", 0, 16), slot("l16_", -1, ci, 3))
    at("l0")
    ts(("L0", 0, LW), ("LL", PAD, PAD + LW), -float(MID), A.add)
    at("const2")
    ms(("ones", 0, 128), 1.0, True)
    ms(("pw", 0, 12), 2.0)
    add(G, "v", (0, 64, 0), [("pw", 0, 12), ("ones", 0, 12)], [("p2", 0, 12)],
        lambda: g.vector.tensor_tensor_scan(X("p2", 0, 12), X("pw", 0, 12), X("ones", 0, 12), 0.5, A.mult, A.mult))
    tt(("pw", 0, 12), ("p2", 0, 12), ("oh", 0, 12), A.mult)
    add(G, "v", (0, 64, 0), [("pw", 0, 12)], [("pw", 12, 13)],
        lambda: g.vector.tensor_reduce(X("pw", 12, 13), X("pw", 0, 12), AxisListType.X, A.add))
    ts(("zc", 0, 144), ("zh", 0, 144), ("pw", 12, 13), A.mult, fast=True)
    ts(("own", 0, 128), ("own0", 0, 128), ("pm", 0, 1), A.add)
    ts(("idp", 0, 128), ("rowp", 0, 128), 0.0, A.is_equal, fast=True)
    ts(("idn", 0, 128), ("rowp", 0, 128), 0.0, A.is_equal, -1.0, A.mult, fast=True)
    ts(("idh", 0, 128), ("rowp", 0, 128), 0.0, A.is_equal, fast=True)
    ms(("kc", 0, 128), (GRANT + MID) / 128.0, True)
    ms(("kd", 0, 128), GRANT / 128.0, True)
    mm(("ps7", 0, 2), ("am", 0, 128), ("ones", 0, 2), True, True)
    ts(("thf", 0, 1), ("thI", 0, 1), 0.5, A.add)
    ts(("thd", 0, 1), ("ps7", 0, 1), 255.5, A.mult, ("thf", 0, 1), A.add)
    ts(("bias", 0, 8), ("p2", 0, 8), ("thd", 0, 1), A.mult, -1.0, A.mult)
    ts(("amh", 0, 128), ("am", 0, 128), 1.0, A.mult, fast=True)
    ts(("am2", 0, 128), ("am", 0, 128), 2.0, A.mult, fast=True)
    at("q0")
    ts(("Q0",) + own(B, V), ("qraw", B, V), 128.0, A.add, fast=True)
    at("fillz")
    if "a" in FILL["NB"] + FILL["NI"]:
        ms(("ub", 0, 1024), 0.0, True)
    for win in sorted(FILL):
        for x, y, q in cut(FILL[win], 0):
            at("fill" + q)
            if q == "v":
                ms((win, x, y), 0.0)
            elif q == "a":
                act((win, x, y), ("ub", 0, y - x), F.Copy)
            else:
                io((win, x, y), [[0, y - x]], 0, 0, False)

    def decide(k, ci):
        ch, P, last = CHUNKS[ci], k % 2, k == RO - 1
        G["c"], G["k"] = str(ci), k
        Qk, e, ah, hb = "Q%d" % k, "e%d" % P, "ah%d" % P, "hb%d" % P
        v0, v1 = ch["c"]
        w0, w1 = v0 // 16, v1 // 16
        win, lst = (Qk, 0, M if ci == 0 else W), (LISTS[ci], 0, w1 - w0)
        L = lambda nm: ("%s%d" % (nm, P), w0, w1)
        S = lambda st: cut(ch.get(st + str(k), ch[st]), v0)
        whole = k == 0 and ci == 0
        at("lay")
        if ci == 0 and k:
            lay("NB", border(k))
        if ci == 1 and k:
            lay("NI", ("LL", LW * k, LW * k + 256))
        for x, y, q in S("hb"):
            at("hb" + q)
            if k == 0:
                gtt((hb, x, y), border(k) if whole else ("L0", 0, LW), offsets(k - 1, ci, 2, x, y), ("mask", x, y), A.mult)
            else:
                gat(q, (hb, x, y), ("NB", 0, M) if ci == 0 else ("NI", 0, 4096), offsets(k - 1, ci, 2, x, y), -float(MID))
        at("xh")
        ext(lst[0], "zn" if k else "zh", hb, v0, v1)
        ts(L("h16_"), lst, 0.0 if whole else float(MID), A.add)
        at("hf")
        if ch["hf"] == "v":
            tc(L("hf"), lst)
        at("ah")
        for x, y, q in S("ah"):
            if q == "v":
                ts((ah, x, y), (Qk,) + own(x, y), -0.5 * 2 ** k, A.add, fast=True)
            else:
                act((ah, x, y), (Qk,) + own(x, y), F.Identity, bias=-0.5 * 2 ** k)
        got = lambda x, y, q: [(max(x, a), min(y, b)) for a, b, c in S("e") if c == q and max(x, a) < min(y, b)]
        at("pre")
        for x, y in halves(v0, v1):
            mm((SUMS[ci], x - v0, y - v0), ("amh" if got(x, y, "a") else "am2", 0, 128), (ah, x, y), True, False)
            for a, b in got(x, y, "v") if got(x, y, "a") else []:
                mm((SUMS[ci], a - v0, b - v0), ("amh", 0, 128), (ah, a, b), False, False)
        for x, y, q in S("e"):
            at("e" + q)
            if q == "v":
                gtt((e, x, y), win, ("h16_%d" % P, x // 16, y // 16), (ah, x, y), A.subtract)
            else:
                gat(q, (e, x, y), win, ("h16_%d" % P, x // 16, y // 16))
        at("sign")
        for x, y in halves(v0, v1):
            mm((SUMS[ci], x - v0, y - v0), ("am", 0, 128), (e, x, y), False, True)
        act(("bits%d" % P, v0, v1), (SUMS[ci], 0, v1 - v0), F.Sign, bias=("bias", k, k + 1))
        at("xc")
        ext(lst[0], "zc", "bits%d" % P, v0, v1)
        ts(L("c16_"), lst, 0.5, A.mult, 2047.5, A.add)
        at("abs")
        for x, y in halves(v0, v1):
            ps, mixed = (DIST[ci], x - v0, y - v0), got(x, y, "v")
            if not mixed:
                mm(ps, ("idn", 0, 128), (ah, x, y), True, False)
            mm(ps, ("idp", 0, 128), (e, x, y), bool(mixed), not mixed or not got(x, y, "a"))
            for a, b in got(x, y, "a") if mixed else []:
                mm((DIST[ci], a - v0, b - v0), ("idn", 0, 128), (ah, a, b), False, True)
        act(("ae%d" % P, v0, v1), (DIST[ci], 0, v1 - v0), F.Abs, scale=float(2.0 ** -k), bias=-0.5)
        at("ok")
        gtt(("veto%d" % P, v0, v1), ("clrs", 0, 4096), L("c16_"), ("ae%d" % P, v0, v1), A.is_lt)
        at("grant")
        mm(lst, ("kd" if whole else "kc", 0, 128), ("ones", 0, w1 - w0), True, False)
        if ch["hf"] == "p":
            ext(lst[0], "zn" if k else "zh", hb, v0, v1, False, False)
        else:
            mm(lst, ("idh", 0, 128), L("hf"), False, False)
        at("xv")
        ext(lst[0], "zv", "veto%d" % P, v0, v1, False)
        tt(slot("y", k, ci, 0), lst, names(k, w0, w1), A.max)
        at("l3")
        tt(slot("y", k, ci, 1), slot("y", k, ci, 0), ("own", w0, w1), A.min)
        if last:
            ts(slot("y", k, ci, 0, 2), slot("y", k, ci, 0, 2), 4095, A.bitwise_and)
            tc(slot("l16_", k, ci, 1), slot("y", k, ci, 1))
            at("names")
            tc(("pout", w0, w1), slot("y", k, ci, 0))
            store(T.yp[:, w0:w1], ("pout", w0, w1))
            return
        if ch.get("l3"):
            ts(slot("y", k, ci, 1), slot("y", k, ci, 1), 4095, A.bitwise_and)
            tc(slot("l16_", k, ci, 1), slot("y", k, ci, 1))
        at("names")
        ts(names(k + 1, w0, w1), slot("y", k, ci, 0), 4095, A.bitwise_and)
        if ci == 0:
            share("LL", "an%d" % (k + 1), PAD + LW * (k + 1), 32, 4)
        at("places")
        places(k + 1, ci, 2 if ch.get("l3") else 1)

    def update(k, ci):
        ch, last = CHUNKS[ci], k == RO - 1
        G["c"], G["k"] = str(ci), k
        Qk, Qn = "Q%d" % k, "Q%d" % (k + 1)
        win = (Qk, 0, M if ci == 0 else W)
        for x, y, q in cut(ch.get("up%d" % k, ch["up"]), ch["c"][0]):
            new, ps = (Qn,) + own(x, y), (SUMS[ci], 0, y - x)
            at("up" + q)
            if q == "v":
                gtt(new, win, offsets(k, ci, 1, x, y), ("ah%d" % (k % 2), x, y), A.add)
            else:
                mm(ps, ("idp", 0, 128), (Qk,) + own(x, y), True, False)
                gat(q, ("ub", x, y), win, offsets(k, ci, 1, x, y))
                mm(ps, ("idp", 0, 128), ("ub", x, y), False, True)
                act(new, ps, F.Identity, bias=-0.5 * 2 ** k)
            if last:
                at("out" + q)
                ts(("yout", x, y), new, 2.0 ** -RO, A.mult, -128.0, A.add, fast=True)
                store(T.yq[:, x:y], ("yout", x, y))
        if not last and ci == 0:
            at("sendq")
            share(Qn, "aq%d" % (k + 1), 0, B, 2)

    for k in range(RO):
        for cis in ([0], range(1, len(CHUNKS))):
            for stage in (decide, update):
                for ci in cis:
                    stage(k, ci)
    return G, nloc[0]


def rank_program(g, core, T, topo):
    if T.rank_of(core) is None:
        return
    G, nloc = build(g, core, T, topo)
    ops = G["ops"]
    if not ORDER:
        ORDER.extend(sorted(improve(ops, schedule(ops), TRIES, WARM, SEED), key=lambda i: i if ops[i]["stage"] == "i load" else len(ops)))
    order = ORDER
    pos = [0] * len(ops)
    for j, i in enumerate(order):
        pos[i] = j
    eng = {"v": g.vector, "a": g.scalar, "p": g.tensor, "g": g, "s": g.sync}
    cnt = {"v": 0, "a": 0, "p": 0, "g": 0}
    known = {q: {} for q in eng}
    tok, snap = {}, {}

    def wait(q, d):
        s, v = tok[d]
        k = known[q]
        if k.get(s, 0) >= v:
            return
        eng[q].wait_ge(T.sem[s], v)
        for a, b in snap[d].items():
            if k.get(a, 0) < b:
                k[a] = b
    for i in order:
        o = ops[i]
        q = o["q"]
        if o["kind"] == "n":
            tok[i] = (o["sem"], o["val"])
            snap[i] = {o["sem"]: o["val"]}
            continue
        for d in sorted(o["edges"], key=lambda d: -pos[d]):
            if q == "p" and ops[d]["q"] == "p" and not o["edges"][d]:
                continue
            if ops[d]["kind"] != "s":
                wait(q, d)
        ins = o["fn"]()
        if o["kind"] == "c":
            cnt[q] += 1
            tok[i] = (QSEM[q], cnt[q])
            ins.then_inc(T.sem[QSEM[q]], 1)
        elif o["kind"] == "d":
            tok[i] = (o["sem"], o["val"])
            ins.then_inc(T.sem[o["sem"]], 16)
        if o["kind"] != "s":
            snap[i] = dict(known[q])
            snap[i][tok[i][0]] = tok[i][1]
    g.wait_ge(T.sem.ls, nloc)
    for i in range(len(ops)):
        if ops[i]["kind"] in ("d", "n"):
            wait("s", i)
    for q in cnt:
        if known["s"].get(QSEM[q], 0) < cnt[q]:
            g.sync.wait_ge(T.sem[QSEM[q]], cnt[q])
